import numpy as np, ml_dtypes
CORES = [5,29,101,125,133,157,229,253]
N = 8
import mx_ref
BF = ml_dtypes.bfloat16
def entries(a):
    return np.ascontiguousarray(a.T).reshape(-1)
def table(e):
    return np.ascontiguousarray(np.reshape(e, (-1, 16)).T).astype(np.int32)
def gcols(t, e):
    v = np.concatenate([t.reshape(8, 16, -1, 4), np.zeros((8, 16, 1, 4), BF)], axis=2)
    return np.ascontiguousarray(np.stack([v[g][:, e[g]] for g in range(8)])).reshape(128, -1)
def gpick(z, e):
    return np.concatenate([z[16 * g:16 * g + 16][:, e[g]] for g in range(8)])
def tile(rs):
    return np.stack(rs, axis=2).reshape(128, -1).astype(BF)
def pick(q, e):
    c = np.concatenate([q[0].reshape(128, -1, 4), np.zeros((128, 1, 4), np.uint8)], axis=1); s = np.concatenate([q[1], np.ones((16, 1), np.uint8)], axis=1)
    return (np.ascontiguousarray(c[:, e].reshape(128, -1)), np.ascontiguousarray(s[:, e]))
def join(*qs):
    return (np.concatenate([q[0] for q in qs], axis=1), np.concatenate([q[1] for q in qs], axis=1))
def put(q, e, v):
    c, s = q[0].reshape(128, -1, 4).copy(), q[1].copy(); c[:, e] = v[0].reshape(128, -1, 4); s[:, e] = v[1]
    return (c.reshape(128, -1), s)
def pk(c, s):
    return (np.ascontiguousarray(c), mx_ref.live(s))
def emit(q):
    return q[0], q[1]
def packed(v, rng):
    q = [mx_ref.quantize(np.ascontiguousarray(v[r])) for r in range(N)]
    return np.stack([a for a, b in q]), np.stack([mx_ref.plane(b, rng) for a, b in q])
def values_of_codes():
    e, c = np.zeros((128, 128, 4), np.float32), np.zeros((128, 2, 4), np.uint8)
    e[np.arange(128), np.arange(128), 0] = 1
    c[:127, :, 0] = np.arange(256).reshape(2, 128).T[:127]
    return mx_ref.matmul(mx_ref.quantize(e.reshape(128, 512).astype(BF)), (c.reshape(128, 8), np.full((16, 2), 127, np.uint8))).T.reshape(-1).astype(np.float64)
CODE_VALUE, SCALE_VALUE = values_of_codes(), 2.0 ** (np.arange(256) - 127.0)
def decode(q):
    return (CODE_VALUE[q[0]].reshape(16, 8, -1, 4) * SCALE_VALUE[q[1]][:, None, :, None] + 0.0).reshape(128, -1).astype(np.float32)
def f(rng, *shape):
    return mx_ref.flush((rng.standard_normal(shape, dtype=np.float32) * np.exp2(rng.integers(-2, 3, shape[:-1] + (1,)))).astype(BF))
def wide(rng, *shape, cols=0):
    v = rng.standard_normal(shape, dtype=np.float32) * np.exp2(rng.integers(-12, 13, shape)).astype(np.float32)
    if cols: v *= np.repeat(np.exp2(rng.integers(-cols, cols + 1, shape[:-2] + (1, shape[-1] // 4))) * (rng.random(shape[:-2] + (1, shape[-1] // 4)) > 0.0625), 4, axis=-1).astype(np.float32)
    return mx_ref.flush(v.astype(BF))
C, H, R = 448, 224, 3
WIDTH = [1, 2, 7, 14, 28, 56, 112, 224]
def big(v):
    v = v.astype(np.float32)
    v[np.abs(v) < np.float32(2.0 ** -16)] = 0
    return v.astype(BF)
def numbers_of(rng):
    return {"x": big(f(rng, N, 128, 4 * C)), "u": np.array(f(rng, N, 128, 512)), "v": np.array(f(rng, N, 128, 512))}
def bases(rng):
    return np.stack([table(rng.permutation(C)) for r in range(N)])
def layers(rng):
    return big(f(rng, N, 128, 2048)).reshape(N, 8, 16, 4, 8, 16, 4)
def weights(rng, w):
    c, s = packed(np.ascontiguousarray(w).reshape(N, 128, 2048), rng)
    return {"wc": c, "ws": s}
def setup_inputs(rng):
    return {**numbers_of(rng), "p": bases(rng), **weights(rng, layers(rng))}
def setup_inputs_ties(rng):
    d = numbers_of(rng)
    p = bases(rng)
    o = rng.permutation(N)
    x = d["x"].astype(np.float32).reshape(N, 8, 16, C, 4)
    n = (N, 8, 8, C, 4)
    x[:, :, 8:] = (1.125 + 0.25 * rng.integers(0, 4, n)) * np.exp2(-1.0 * rng.integers(8, 15, n)) * rng.choice([-1.0, 1.0], n)
    x[:, :, 8, :, 0] = 1.96875
    x[:, :, :8] = 0
    u = d["u"].reshape(N, 128, 128, 4)
    u[:, :, ::16] = 0
    for r in range(N):
        if o[r] % 2 == 1: x[r, :, 0, :, 0] = rng.integers(0, 4, (8, C))
        else: x[r, :, 0, :, 0] = rng.integers(0, 7, (1, C)) + rng.integers(0, 2, (8, C))
        for h in range(0, 128, 16): u[r, h, h, 0] = 0.0 if o[r] == 0 else -1.0 if o[r] == 1 else 1.0
        if o[r] == 0:
            x[r, 7, 0, :, 0] = 0
            x[r, 7, 0, p[r, 0, 0], 0] = 1
            u[r, 112, 112, 0] = 1.0
    w = layers(rng)
    w[:, :, :, :, :, :8] = 0
    return {"x": x.reshape(N, 128, 4 * C).astype(BF), "u": u.reshape(N, 128, 512), "v": d["v"], "p": p, **weights(rng, w)}
def setup_inputs_near(rng):
    d = numbers_of(rng)
    x = d["x"].astype(np.float32).reshape(N, 8, 16, C, 4)
    u = d["u"].reshape(N, 128, 128, 4)
    o = rng.permutation(N) % 4
    x[:, :, 0] = 0
    x[:, :, 8:] = 0
    u[:, :, ::16] = 0
    for r in range(N):
        k = 1.0 if o[r] == 0 else 2.0 ** -30
        if o[r] < 3:
            s = rng.integers(0, 252, (1, C)) + rng.integers(0, 4, (8, C))
            for i in range(2): x[r, :, 8 + i] = ((s[:, :, None] >> (4 * i + np.arange(4))) & 1) * np.exp2(4 * i + np.arange(4) - 23.0)
            if o[r] < 2:
                x[r, :, 0, :, 0] = rng.choice([-1.0, 1.0], C)
                x[r, :, 11, :, 0] = 2.0 ** -10
            for g in rng.permutation(8)[:4]: x[r, g, 0, rng.integers(C), 0] = 2.0 ** 29 * rng.choice([-1.0, 1.0])
        else:
            for i in (10, 12): x[r, :, i, :, 0] = (1.0 + 0.125 * rng.integers(0, 2, (8, C))) * 2.0 ** -30
        for h in range(0, 128, 16):
            if o[r] < 3:
                u[r, h, h, 0] = k
                u[r, h + 8:h + 10, h] = k
                u[r, h + 11, h, 0] = k
            else:
                a = rng.choice([-1.0, 1.0])
                u[r, h + 10, h, 0] = 1.125 * k * a
                u[r, h + 12, h, 0] = -k * a
    w = layers(rng)
    for i in (0, 8, 9, 10, 11, 12, 13, 14, 15):
        w[:, :, i] = 0
        w[:, :, :, :, :, i] = 0
    return {"x": x.reshape(N, 128, 4 * C).astype(BF), "u": u.reshape(N, 128, 512), "v": d["v"], "p": bases(rng), **weights(rng, w)}
def setup_inputs_huge(rng):
    d = numbers_of(rng)
    o = rng.permutation(N)
    x = 0.6 + 0.06 * rng.random((N, 8, 16, C, 4)) + 0.03 * rng.random((N, 1, 1, C, 1))
    a = 1.0 - 0.1 * rng.random((N, 128, 8, 4))
    for r in range(N):
        if o[r] < N // 2: a[r] *= -1.0
        else:
            x[r] *= rng.choice([-1.0, 1.0], (1, 1, C, 1))
            a[r] *= rng.choice([-1.0, 1.0], (1, 8, 1))
    u = d["u"].reshape(N, 128, 128, 4)
    u[:, :, ::16] = (2.0 ** 30 * a).astype(np.float32).astype(BF)
    w = np.zeros((N, 128, 4, 128, 4), np.float32)
    i = np.arange(128)
    for b in range(4): w[:, i, b, i, b] = -4
    return {"x": (2.0 ** 30 * x).astype(np.float32).reshape(N, 128, 4 * C).astype(BF), "u": u.reshape(N, 128, 512), "v": d["v"], "p": bases(rng), **weights(rng, w.astype(BF))}
def setup_inputs_ends(rng):
    v = np.array(f(rng, N, 128, 512))
    o = rng.permutation(N) % 4
    x, u = np.zeros((N, 128, C, 4), np.float32), np.zeros((N, 128, 128, 4), np.float32)
    w, e = np.zeros((N, 128, 4, 128, 4), np.float32), []
    i = np.arange(128)
    for r in range(N):
        c = rng.choice([-1.0, 1.0], (1, C, 1))
        a = rng.choice([-1.0, 1.0], (1, 128, 1))
        if o[r] == 0:
            x[r] = 2.0 ** 30
            x[r, 64:] *= rng.choice([0.5, 1.0], (64, C, 4))
            x[r, 64:, ::4] = 2.0 ** 30
            u[r] = -2.0 ** 30
            u[r, 64:, :64] = 0
        elif o[r] == 1:
            x[r] = 2.0 ** 30 * c
            u[r] = 2.0 ** 30 * a
        elif o[r] == 2:
            x[r] = 2.0 ** -29 * rng.choice([-1.0, 1.0], (128, C, 4))
            u[r] = 2.0 ** -30 * rng.choice([-1.0, 1.0], (128, 128, 4))
        else:
            x[r] = 2.0 ** -29 * c
            u[r] = 2.0 ** -30 * a
        if o[r] > 1:
            for b in range(4): w[r, i, b, i, b] = 2.0 ** -20
        e.append(table(np.arange(C) if o[r] % 2 == 0 else C - 1 - np.arange(C)))
    v = (np.where(v < 0, -1.0, 1.0) * np.where(rng.permutation(N) % 2, 2.0 ** -30, 2.0 ** 30)[:, None, None]).astype(np.float32).astype(BF)
    return {"x": x.reshape(N, 128, 4 * C).astype(BF), "u": u.reshape(N, 128, 512).astype(BF), "v": v, "p": np.stack(e), **weights(rng, w.astype(BF))}
def setup_inputs_spread(rng):
    d = setup_inputs(rng)
    d["x"] = big(wide(rng, N, 128, 4 * C, cols=6))
    return d
def check_inputs(d):
    bad = []
    for k in ("x", "u", "v"):
        a = np.abs(d[k].astype(np.float32))
        if not (np.isfinite(a).all() and ((a == 0) | (a >= 2.0 ** -30) & (a <= 2.0 ** 30)).all()): bad.append("a value of " + k)
    none, least, most = [emit(mx_ref.quantize(np.full((128, 16), k, np.float32).astype(BF)))[1][0, 0] for k in (0.0, 2.0 ** -30, 2.0 ** 30)]
    for r in range(N):
        if not np.array_equal(np.sort(d["p"][r].reshape(-1)), np.arange(C)): bad.append("p: not every column once")
        if ((d["wc"][r] == 0x7F) | (d["wc"][r] == 0xFF)).any(): bad.append("wc: a code that is no number")
        s = mx_ref.live(d["ws"][r])
        if ((s != none) & ((s < least) | (s > most))).any(): bad.append("ws: a scale out of range")
    return bad
def reference(x, u, v, p, wc, ws):
    qu = [mx_ref.quantize(u[r]) for r in range(N)]
    lay = [pk(wc[r], ws[r]) for r in range(N)]
    now = [x[r] for r in range(N)]
    base = [entries(p[r]) for r in range(N)]
    order = np.zeros((N, 8, C), np.int64)
    for t in range(R):
        own, sent = [], []
        for r in range(N):
            q = mx_ref.quantize(now[r])
            own.append(decode(q))
            s = mx_ref.matmul(qu[r], q)[::16] + np.float32(0.0)
            o = base[r]
            for g in range(8):
                key = np.maximum.accumulate(s[g][o].reshape(-1, WIDTH[g]), axis=1).reshape(-1, 2 * WIDTH[g])
                o = np.take_along_axis(o.reshape(-1, 2 * WIDTH[g]), np.argsort(key, axis=1, kind="stable"), axis=1).reshape(-1)
                order[r, g] = o
            base[r] = o
            a = own[r].astype(BF)
            z = (gcols(a, order[r, :, :H]).astype(np.float32) + gcols(a, order[r, :, H:]).astype(np.float32)) * np.float32(0.5)
            sent.append(mx_ref.quantize(z.astype(BF)))
        for r in range(N):
            q = sent[(r - 1) % N]
            place = np.argsort(order[r], axis=1) % H
            now[r] = tile([gpick(mx_ref.matmul(pick(lay[r], np.arange(128 * b, 128 * b + 128)), q), place) * np.float32(0.03125) + own[r][:, b::4] for b in range(4)])
    y, od = np.zeros((N, 128, C), np.float32), np.zeros((N, 8, C), np.float32)
    oc, osc = np.zeros((N, 128, 4 * C), np.uint8), np.zeros((N, 16, C), np.uint8)
    for r in range(N):
        q = mx_ref.quantize(now[r])
        y[r] = mx_ref.matmul(mx_ref.quantize(v[r]), q)
        od[r] = order[r]
        oc[r], osc[r] = emit(q)
    return {"y": y, "od": od, "oc": oc, "osc": osc}

@@ -1,0 +1,566 @@
+from concourse.bass import DstId, RemoteDMATransfer
+from concourse.mybir import dt, AluOpType, ActivationFunctionType
+
+OP = AluOpType
+AF = ActivationFunctionType
+ROUNDS, C, HALF = 3, 448, 224
+BIG = 1e29
+TW = 536
+
+SCRATCH = {}
+
+
+def _sb(name, n, ty="float32"):
+    SCRATCH[name] = ("sbuf", [128, n], ty)
+
+
+def _mx(c, s, n):
+    _sb(c, n, "float8_e4m3fn_x4")
+    _sb(s, n, "uint8")
+
+
+for _n, _w in (("xt", 1792), ("xn", 1792), ("ut", 512), ("vt", 512), ("one", 576), ("qtr", 576), ("eb", 516), ("cb", 576), ("cl", 2048),
+               ("G", TW), ("WQ", TW), ("W1", TW), ("W2", TW), ("FB", 896), ("HB", 1792), ("ZT", 896), ("gm", 8)):
+    _sb(_n, _w, "bfloat16")
+for _n, _w in (("MR", 384), ("MT", 384), ("KF", 28), ("KL", 8), ("BQ", 672), ("BF", 2 * C), ("CUR", 128), ("CURF", 512), ("KEY", 128),
+               ("KEYF", 512), ("TQ", 128), ("TF", 512), ("TS", 8), ("MC", 128), ("MC2", 128), ("MCF", 512), ("MCG", 512), ("TMP", 256),
+               ("DR", 1664), ("XL", 8), ("YL", 8), ("XK", 8), ("DK", 8), ("XF", 28), ("YF", 28), ("CK", 28), ("CT", 28), ("SIG", 480),
+               ("TT", 896), ("CA", 28), ("CB", 28), ("CD", 28), ("KT", 28), ("IOT", C), ("COL", 3 * C), ("OD", 480), ("GZ", 896),
+               ("PB", 896), ("RG", 2 * C), ("yb", C)):
+    _sb(_n, _w)
+for _n, _w in (("pi", 28), ("ii", 84), ("ML", 8), ("MF", 28)):
+    _sb(_n, _w, "int32")
+for _n, _w in (("LL", 8), ("LF", 28), ("RL", 28), ("RM", 28), ("R2", 28), ("ZL", 28), ("PL", 28), ("CW", 28), ("IC", 28), ("UL", 64)):
+    _sb(_n, _w, "uint16")
+_mx("qu", "su", 128)
+_mx("qB", "sB", 1024)
+_mx("qv", "pv", 128)
+_mx("wq", "wp", 512)
+_mx("qcb", "scb", 144)
+_mx("qcl", "scl", 512)
+_mx("qe", "se", 512)
+_mx("ga", "gas", 132)
+_mx("gb", "gbs", 132)
+_mx("wa", "was", 132)
+_mx("wb", "wbs", 132)
+for _t in range(ROUNDS + 1):
+    _mx("qx%d" % _t, "sx%d" % _t, C)
+    _mx("qp%d" % _t, "sp%d" % _t, C)
+for _t in range(ROUNDS):
+    _mx("zc%d" % _t, "zs%d" % _t, HALF)
+    _mx("lc%d" % _t, "ls%d" % _t, HALF)
+    _mx("hc%d" % _t, "hs%d" % _t, HALF // 2)
+SCRATCH["ps"] = ("psum", [128, 4096], "float32")
+
+SEMAPHORES = (["sv", "st", "ss", "sg", "snd", "dx", "dp", "du", "dw", "dv", "dy", "dc", "dd", "dq"]
+              + ["%s%d" % (_a, _t) for _a in ("rc", "rs", "lz") for _t in range(ROUNDS)])
+
+
+def _relays(topo, src, dst):
+    ok = [c for c in topo.cores_of(src) if c != src and topo.may_write(c, dst)]
+    near = [c for c in ok if topo.die(c) == topo.die(src)]
+    far = [c for c in ok if topo.die(c) != topo.die(src)]
+    return [near[0], far[0]]
+
+
+def _bits(engines):
+    m = 0
+    for e in engines:
+        m |= 1 << e
+    return m
+
+
+def _relay_program(g, core, T, topo):
+    n = len(T.cores)
+    for r in range(n):
+        dst = T.cores[(r + 1) % n]
+        rel = _relays(topo, T.cores[r], dst)
+        if core not in rel:
+            continue
+        h = rel.index(core)
+        a, b = h * HALF // 2, (h + 1) * HALF // 2
+        rid, pid = topo.addr(dst, core)
+        m = topo.mask(core, dst)
+        k = len(topo.engines(core, dst))
+        half = len(topo.engines(T.cores[r], core)) // 2
+        for t in range(ROUNDS):
+            g.wait_ge(T.sem["rc%d" % t], half)
+            g.remote_dma(T["lc%d" % t][:, a:b].bitcast(dt.uint8), T["hc%d" % t][:, :].bitcast(dt.uint8), T.sem["lz%d" % t], T.sem.snd, pid, rid, m)
+            g.wait_ge(T.sem["rs%d" % t], half)
+            g.remote_dma(T["ls%d" % t][:, a:b], T["hs%d" % t][:, :], T.sem["lz%d" % t], T.sem.snd, pid, rid, m)
+        g.wait_ge(T.sem.snd, 2 * k * ROUNDS)
+
+
+def rank_program(g, core, T, topo):
+    rank = T.rank_of(core)
+    if rank is None:
+        _relay_program(g, core, T, topo)
+        return
+    Q = {"v": g.vector, "t": g.tensor, "s": g.scalar, "g": g, "y": g.sync}
+    ESEM = {"v": "sv", "t": "st", "s": "ss", "g": "sg"}
+    count = {"sv": 0, "st": 0, "ss": 0, "sg": 0}
+    seen = {}
+    hist = {}
+
+    def A(name, c0, c1, st=1, p0=0, p1=128):
+        t = T[name]
+        if st == 1:
+            ap = t[:, c0:c1] if (p0, p1) == (0, 128) else t[p0:p1, c0:c1]
+        else:
+            ap = t[:, c0:c1:st] if (p0, p1) == (0, 128) else t[p0:p1, c0:c1:st]
+        return (ap, [(name, p0, p1, c0, c1)])
+
+    def ps(bank, c0, c1, st=1, p0=0, p1=128):
+        x = A("ps", 512 * bank + c0, 512 * bank + c1, st, p0, p1)
+        return (x[0], [("ps%d" % bank, 0, 128, 0, 512)])
+
+    def ind(win, off):
+        return (win[0].indirect(off[0]), win[1] + off[1])
+
+    def bc(x):
+        return (x[0].bitcast(dt.uint8), x[1])
+
+    def u32(x):
+        return (x[0].bitcast(dt.uint32), x[1])
+
+    def wait(q, sem, val):
+        if seen.get((q, sem), 0) < val:
+            Q[q].wait_ge(T.sem[sem], val)
+            seen[(q, sem)] = val
+
+    def hazards(q, reads, writes):
+        need = {}
+        for regs, w in ((reads, False), (writes, True)):
+            for (n, p0, p1, c0, c1) in regs:
+                bank = n[:2] == "ps"
+                for (eq, sem, val, ew, a0, a1, b0, b1) in hist.get(n, ()):
+                    if a0 >= p1 or p0 >= a1 or b0 >= c1 or c0 >= b1:
+                        continue
+                    if bank and eq == q and (q == "t" or not ew):
+                        continue
+                    if not bank and not w and not ew:
+                        continue
+                    need[sem] = max(need.get(sem, 0), val)
+        for sem in need:
+            wait(q, sem, need[sem])
+
+    def note(q, sem, val, reads, writes):
+        for regs, w in ((reads, False), (writes, True)):
+            for (n, p0, p1, c0, c1) in regs:
+                h = hist.setdefault(n, [])
+                if w:
+                    h[:] = [e for e in h if not (p0 <= e[4] and e[5] <= p1 and c0 <= e[6] and e[7] <= c1 and e[0] == q)]
+                h[:] = [e for e in h if not (e[0] == q and e[1] == sem and e[3] == w and e[4:] == (p0, p1, c0, c1))]
+                h.append((q, sem, val, w, p0, p1, c0, c1))
+
+    def do(q, call, outs, ins):
+        reads = [r for x in ins for r in x[1]]
+        writes = [r for x in outs for r in x[1]]
+        hazards(q, reads, writes)
+        sem = ESEM[q]
+        count[sem] += 1
+        call().then_inc(T.sem[sem], 1)
+        note(q, sem, count[sem], reads, writes)
+
+    def dmas(q, pairs, sem):
+        for out, in_ in pairs:
+            hazards(q, in_[1], out[1])
+        for out, in_ in pairs:
+            Q[q].dma_start(out[0], in_[0]).then_inc(T.sem[sem], 16)
+        count[sem] = count.get(sem, 0) + 16 * len(pairs)
+        for out, in_ in pairs:
+            note("d" + sem, sem, count[sem], in_[1], out[1])
+
+    def tt(out, a, b, op):
+        do("v", lambda: g.vector.tensor_tensor(out[0], a[0], b[0], op), [out], [a, b])
+
+    def ts(out, a, s1, op0, s2=None, op1=None):
+        ins = [a] + [x for x in (s1, s2) if isinstance(x, tuple)]
+        v1 = s1[0] if isinstance(s1, tuple) else s1
+        v2 = s2[0] if isinstance(s2, tuple) else s2
+        if op1 is None:
+            do("v", lambda: g.vector.tensor_scalar(out[0], a[0], v1, None, op0), [out], ins)
+        else:
+            do("v", lambda: g.vector.tensor_scalar(out[0], a[0], v1, v2, op0, op1), [out], ins)
+
+    def cp(out, a):
+        do("v", lambda: g.vector.tensor_copy(out[0], a[0]), [out], [a])
+
+    def act(out, a, scale=1.0):
+        if scale == 1.0:
+            do("s", lambda: g.scalar.activation(out[0], a[0], AF.Copy), [out], [a])
+        else:
+            do("s", lambda: g.scalar.activation(out[0], a[0], AF.Copy, scale=scale), [out], [a])
+
+    def pick(qo, so, o, qi, si, w, off):
+        act(A(so, *o), ind(A(si, 0, w), off))
+        src = A(qi, 0, w)
+        do("v", lambda: g.vector.tensor_copy(u32(A(qo, *o))[0], u32(src)[0].indirect(off[0])), [A(qo, *o)], [src, off])
+
+    def scatter(win, off, vals):
+        do("v", lambda: g.vector.tensor_copy(win[0].indirect(off[0]), vals[0]), [win], [vals, off])
+
+    def scan(out, d0, d1):
+        do("v", lambda: g.vector.tensor_tensor_scan(out[0], d0[0], d1[0], -BIG, OP.min, OP.max), [out], [d0, d1])
+
+    def tr(out, a):
+        do("v", lambda: g.vector.transpose(out[0], a[0]), [out], [a])
+
+    def fill(x, val):
+        do("v", lambda: g.vector.memset(x[0], val), [x], [])
+
+    def quant(c, s, a):
+        do("v", lambda: g.vector.quantize_mx(c[0], s[0], a[0]), [c, s], [a])
+
+    def mm(out, w, ws, x, xs, start=True, stop=True):
+        do("t", lambda: g.tensor.matmul_mx(out[0], w[0], ws[0], x[0], xs[0], start, stop), [out], [w, ws, x, xs])
+
+    def aff(out, in_, pattern, op, val, base, cm):
+        do("g", lambda: g.affine_select(out[0], in_[0], pattern, op, val, base, cm), [out], [in_])
+
+    def iota(out, pattern, base, cm):
+        do("g", lambda: g.iota(out[0], pattern, base, cm, allow_small_or_imprecise_dtypes=True), [out], [])
+
+    def ext(ap):
+        return (ap, [])
+
+    dmas("s", [(A("pi", 0, 28, 1, 16 * h, 16 * h + 16), ext(T.p[:, :])) for h in range(0, 8)], "dp")
+    dmas("y", [(A("ut", 0, 512), ext(T.u[:, :]))], "du")
+    dmas("y", [(A("xt", 0, 1792), ext(T.x[:, :]))], "dx")
+    dmas("y", [(bc(A("wq", 0, 512)), ext(T.wc[:, :])), (A("wp", 0, 512), ext(T.ws[:, :]))], "dw")
+    dmas("y", [(A("vt", 0, 512), ext(T.v[:, :]))], "dv")
+
+    for h in range(8):
+        fill(A("UL", 8 * h, 8 * h + 8), 16 * h)
+    fill(A("qtr", 0, 576), 0.25)
+    fill(A("one", 0, 576), 1.0)
+    iota(A("ii", 0, 28), [[16, 28]], 0, 0)
+    iota(A("ii", 28, 56), [[0, 28]], 0, 1)
+    aff(A("cb", 0, 576), A("qtr", 0, 576), [[0, 9], [1, 16], [-1, 4]], OP.is_equal, 0.0, 0, 0)
+    fill(A("CUR", 0, 128), -BIG)
+    fill(A("MC", 0, 128), 0.0)
+    fill(A("G", 0, TW), 0.0)
+    fill(A("WQ", 0, TW), 0.0)
+    quant(A("qu", 0, 128), A("su", 0, 128), A("ut", 0, 512))
+    cp(A("PL", 0, 28), A("pi", 0, 28))
+    MASKS = {"m0": (0, 0, 1, 1.0), "lo": (1, 0, 16, 1.0), "hi": (2, 16, 32, 1.0), "h16": (3, 16, 32, 16.0),
+             "b0": (4, 7, 14, 1.0), "b1": (5, 0, 7, -1.0), "b2": (6, 21, 28, 1.0), "b3": (7, 14, 21, -1.0),
+             "c0": (8, 14, 28, 1.0), "c1": (9, 0, 14, -1.0), "p": (10, 0, 28, 1.0), "n": (11, 0, 28, -1.0)}
+
+    def mask(k):
+        j = MASKS[k][0]
+        return A("MT", 32 * j, 32 * j + 1)
+
+    def phys(y, m, x):
+        ts(m, x, 1.0 / 7.0, OP.mult, -27.0 / 56.0, OP.add)
+        tt(y, m, x, OP.add)
+
+    def repeat_u(h):
+        pick("qB", "sB", (128 * h, 128 * h + 128), "qu", "su", 128, A("UL", 8 * h, 8 * h + 8))
+
+    def more_constants():
+        fill(A("MR", 0, 384), 0.0)
+        for k in MASKS:
+            j, a, b, val = MASKS[k]
+            fill(A("MR", 32 * j + a, 32 * j + b), val)
+        tr(A("MT", 0, 384), A("MR", 0, 384))
+        ts(A("ii", 56, 84), A("ii", 28, 56), 15, OP.bitwise_and)
+        tt(A("KF", 0, 28), A("ii", 0, 28), A("ii", 56, 84), OP.add)
+        ts(A("KF", 0, 28), A("KF", 0, 28), 0.25, OP.mult)
+        phys(A("KL", 0, 7), A("ML", 0, 7), A("KF", 0, 7))
+        tt(A("DK", 0, 7), A("KF", 0, 7), A("KL", 0, 7), OP.subtract)
+        fill(A("cl", 0, 2048), 0.0)
+        for k in range(4):
+            s = 4 * ((16 - 4 * k) % 16)
+            for a in range(4):
+                cp(A("cl", 512 * k + 128 * a, 512 * k + 128 * a + 128, 1, 32 * a, 32 * a + 32), A("cb", s + 128 * a, s + 128 * a + 128, 1, 32 * a, 32 * a + 32))
+
+    def never(name, a, b, val):
+        aff(A(name, a, b), A("IOT", 0, b - a), [[0, b - a]], OP.is_equal, val, 1, 0)
+
+    iota(A("IOT", 0, C), [[1, C]], 0, 0)
+    never("DR", 0, 320, BIG)
+    never("DR", 320, 640, BIG)
+    aff(A("gm", 0, 8), A("one", 0, 8), [[-16, 8]], OP.is_ge, 0.0, 0, 1)
+    aff(A("eb", 0, 516), A("one", 0, 516), [[1, 516]], OP.is_equal, 0.0, -3, -4)
+    for c0 in (640, 984, 1328):
+        never("DR", c0, min(c0 + 344, 1664), BIG)
+    never("CURF", 0, 256, -BIG)
+    never("CURF", 256, 512, -BIG)
+    for name in ("W1", "W2", "SIG", "OD"):
+        n = SCRATCH[name][1][1]
+        iota(A(name, 0, n), [[0, n]], 0, 0)
+    BLK = [1, 2, 7, 14, 28, 56, 112, 224]
+
+    def resets(late):
+        if late:
+            fill(A("DR", 640, 1152, 128), -BIG)
+            fill(A("DR", 1152, 1664, 256), -BIG)
+            return
+        fill(A("DR", 0, 128, 2), -BIG)
+        for s in (0, 7, 14, 21):
+            fill(A("DR", 128 + s, 256, 32), -BIG)
+        for s in (0, 14):
+            fill(A("DR", 256 + s, 384, 32), -BIG)
+        fill(A("DR", 384, 512, 32), -BIG)
+        fill(A("DR", 512, 640, 64), -BIG)
+
+    LB, FK = 4, 5
+
+    def counts(bank, ca, cas, cb_, cbs, local, start=True, stop=True):
+        for i, k in enumerate((0, 2, 1, 3)):
+            s = (16 - 4 * k) % 16
+            w, ws = (A("qcl", 128 * k, 128 * k + 128), A("scl", 128 * k, 128 * k + 128)) if local else (A("qcb", s, s + 128), A("scb", s, s + 128))
+            c, cs = (ca, cas) if k in (0, 2) else (cb_, cbs)
+            o = 2 if k in (2, 3) else 0
+            mm(ps(bank, 0, 128), w, ws, A(c, o, o + 128), A(cs, o, o + 128), start and i == 0, stop and i == 3)
+
+    def quant2(tile, ca, cas, cb_, cbs):
+        quant(A(ca, 0, 132), A(cas, 0, 132), A(tile, 0, 528))
+        quant(A(cb_, 0, 132), A(cbs, 0, 132), A(tile, 4, 532))
+
+    def wrap(dst, row):
+        tr(A("TT", 0, C), A(row, 0, C))
+        tr(A("TT", C, 2 * C), A(row, 16, 16 + C))
+        ts(A("CA", 0, 28), A("TT", 0, 896, 32), mask("lo"), OP.mult)
+        ts(A("CB", 0, 28), A("TT", 16, 896, 32), mask("hi"), OP.mult)
+        tt(A("CD", 0, 28), A("CA", 0, 28), A("CB", 0, 28), OP.add)
+        cp(A(dst, 0, 28, 2), A("CD", 0, 14))
+        cp(A(dst, 1, 28, 2), A("CD", 14, 28))
+
+    SBANK = [0, 1, 2, 3, 6, 7, 0, 1]
+    DBANK = [2, 3, 6, 7]
+    dst = T.cores[(rank + 1) % len(T.cores)]
+    rel = _relays(topo, core, dst)
+    eng = topo.engines(core, rel[0])
+    cut = [eng[:len(eng) // 2], eng[len(eng) // 2:]]
+    landed = 2 * sum(len(topo.engines(r, core)) for r in _relays(topo, T.cores[rank - 1], core))
+
+    for t in range(ROUNDS):
+        qx, sx, qp, sp = "qx%d" % t, "sx%d" % t, "qp%d" % t, "sp%d" % t
+        quant(A(qx, 0, C), A(sx, 0, C), A("xt" if t == 0 else "xn", 0, 1792))
+        for i in range(2):
+            pick(qp, sp, (HALF * i, HALF * i + HALF), qx, sx, C, A("PL", 14 * i, 14 * i + 14))
+        if t == 0:
+            repeat_u(0)
+        for i, bank in enumerate((0, 4)):
+            o = (HALF * i, HALF * i + HALF)
+            mm(ps(bank, 0, HALF), A("qB", 0, 128), A("sB", 0, 128), A(qp, *o), A(sp, *o))
+            for a in (2 * i, 2 * i + 1):
+                out, in_ = A("BQ", 0, 112, 1, 32 * a, 32 * a + 32), ps(bank, 112 * (a % 2), 112 * (a % 2) + 112, 1, 32 * a, 32 * a + 32)
+                (act if i == 0 else cp)(out, in_)
+
+        def scores(h):
+            mm(ps(SBANK[h], 0, C), A("qB", 128 * h, 128 * h + 128), A("sB", 128 * h, 128 * h + 128), A(qp, 0, C), A(sp, 0, C))
+
+        def evac(h):
+            if h > 5:
+                act(A("BF", C * (h - 6), C * (h - 5)), ps(SBANK[h], 0, C))
+                return
+            for a in range(4):
+                act(A("BQ", 112 * h, 112 * h + 112, 1, 32 * a, 32 * a + 32), ps(SBANK[h], 112 * a, 112 * a + 112, 1, 32 * a, 32 * a + 32))
+
+        def unpack(b):
+            mm(ps(DBANK[b], 0, C), A("qe", 128 * b, 128 * b + 128), A("se", 128 * b, 128 * b + 128), A(qp, 0, C), A(sp, 0, C))
+            act(A("HB", C * b, C * b + C), ps(DBANK[b], 0, C), 0.5)
+            if b < 2:
+                act(A("FB", C * b, C * b + C), ps(DBANK[b], 0, C))
+
+        if t == 0:
+            more_constants()
+            repeat_u(1)
+        ts(A("LL", 0, 7), A("KL", 0, 7), 4.0, OP.mult)
+        if t == 0:
+            quant(A("qcb", 0, 144), A("scb", 0, 144), A("cb", 0, 576))
+            for k in range(4):
+                quant(A("qcl", 128 * k, 128 * k + 128), A("scl", 128 * k, 128 * k + 128), A("cl", 512 * k, 512 * k + 512))
+        scores(1)
+        evac(1)
+
+        def background(lev):
+            if t == 0:
+                if lev == 0:
+                    resets(False)
+                if lev < 6:
+                    repeat_u(lev + 2)
+                if lev == 1:
+                    for b in range(4):
+                        quant(A("qe", 128 * b, 128 * b + 128), A("se", 128 * b, 128 * b + 128), A("eb", 3 - b, 515 - b))
+                    act(A("COL", 0, C), ind(A("IOT", 0, C), A("PL", 0, 28)))
+                if lev == 5:
+                    resets(True)
+                    quant(A("qv", 0, 128), A("pv", 0, 128), A("vt", 0, 512))
+            scores(lev + 2)
+            evac(lev + 2)
+            if lev in (4, 5):
+                unpack(2 * (lev - 4))
+                unpack(2 * (lev - 4) + 1)
+
+        def keep(lev):
+            f = ps(FK, 0, 112, 4)
+            ts(A("CT", 0, 28), f, A("gm", lev, lev + 1), OP.mult)
+            if lev < 5:
+                tt(A("XF", 0, 28), f, A("XF" if lev else "KF", 0, 28), OP.add)
+            tt(A("CK", 0, 28), A("CK" if lev else "KF", 0, 28), A("CT", 0, 28), OP.add)
+
+        for lev in range(6):
+            scatter(A("CUR", 0, 128), A("LL", 0, 7), A("BQ", 112 * lev, 112 * lev + 112))
+            first = None
+            if lev == 0:
+                tt(A("MC", 0, 128, 2), A("CUR", 1, 128, 2), A("CUR", 0, 128, 2), OP.is_lt)
+                ts(A("MC", 1, 128, 2), A("MC", 0, 128, 2), -1.0, OP.mult)
+                first = mask("m0")
+            else:
+                scan(A("KEY", 0, 128), A("DR", 128 * (lev - 1), 128 * lev), A("CUR", 0, 128))
+            if lev == 1:
+                k = [A("KEY", i, 128, 4) for i in range(4)]
+                c = [A("TMP", 32 * i, 32 * i + 32) for i in range(4)]
+                tt(c[0], k[0], k[2], OP.is_gt)
+                tt(c[1], k[0], k[3], OP.is_gt)
+                tt(c[2], k[1], k[2], OP.is_gt)
+                tt(c[3], k[1], k[3], OP.is_gt)
+                ts(A("TMP", 128, 256), A("TMP", 0, 128), -1.0, OP.mult)
+                tt(A("MC", 0, 128, 4), c[0], c[1], OP.add)
+                tt(A("MC", 1, 128, 4), c[2], c[3], OP.add)
+                n = [A("TMP", 128 + 32 * i, 160 + 32 * i) for i in range(4)]
+                tt(A("MC", 2, 128, 4), n[0], n[2], OP.add)
+                tt(A("MC", 3, 128, 4), n[1], n[3], OP.add)
+                first = mask("m0")
+            if lev > 1:
+                tr(A("TQ", 0, 128), A("KEY", 0, 128))
+                one = lambda b: A("TQ", 32 * b, 32 * b + 1)
+                if lev in (2, 3):
+                    w = BLK[lev]
+                    for b in range(4):
+                        for j in range(28 // w):
+                            a = 32 * b + w * j
+                            ts(A("MC", a, a + w), A("KEY", a, a + w), one(b), OP.is_lt if j % 2 else OP.is_gt, mask(("b%d" if lev == 2 else "c%d") % j), OP.mult)
+                elif lev == 4:
+                    for b in range(4):
+                        a = 32 * b
+                        ts(A("MC", a, a + 32), A("KEY", a, a + 32), one(b ^ 1), OP.is_lt if b % 2 else OP.is_gt, mask("n" if b % 2 else "p"), OP.mult)
+                else:
+                    for i, m in enumerate(("MC", "MC2")):
+                        ts(A(m, 0, 64), A("KEY", 0, 64), one(2 + i), OP.is_gt, mask("p"), OP.mult)
+                        ts(A(m, 64, 128), A("KEY", 64, 128), one(i), OP.is_lt, mask("n"), OP.mult)
+                    tt(A("MC", 0, 128), A("MC", 0, 128), A("MC2", 0, 128), OP.add)
+            back = ind(A("MC", 0, 128), A("LL", 0, 7))
+            if first is not None:
+                ts(A("G", 0, 112), back, first, OP.mult)
+            else:
+                cp(A("G", 0, 112), back)
+            if lev < 5:
+                quant2("G", "ga", "gas", "gb", "gbs")
+                counts(LB, "ga", "gas", "gb", "gbs", True)
+            for a in range(4):
+                (cp if a < 2 or lev == 5 else act)(A("WQ", 112 * a, 112 * a + 112, 1, 32 * a, 32 * a + 32), A("G", 0, 112, 1, 32 * a, 32 * a + 32))
+            if lev > 0:
+                keep(lev - 1)
+            if lev == 4:
+                tt(A("XK", 0, 7), A("XL", 0, 7), A("DK", 0, 7), OP.add)
+            quant2("WQ", "wa", "was", "wb", "wbs")
+            counts(FK, "wa", "was", "wb", "wbs", False)
+            if lev < 5:
+                loc = ps(LB, 0, 28, 4)
+                if lev < 4:
+                    tt(A("XL", 0, 7), loc, A("XL" if lev else "KL", 0, 7), OP.add)
+                    ts(A("LL", 0, 7), A("XL", 0, 7), 4.0, OP.mult)
+                else:
+                    tt(A("XL", 0, 7), loc, A("XK", 0, 7), OP.add)
+                    phys(A("YL", 0, 7), A("ML", 0, 7), A("XL", 0, 7))
+                    ts(A("LL", 0, 7), A("YL", 0, 7), 4.0, OP.mult)
+            background(lev)
+
+        for lev in (6, 7):
+            tt(A("XF", 0, 28), ps(FK, 0, 112, 4), A("XF", 0, 28), OP.add)
+            phys(A("YF", 0, 28), A("MF", 0, 28), A("XF", 0, 28))
+            ts(A("LF", 0, 28), A("YF", 0, 28), 4.0, OP.mult)
+            scatter(A("CURF", 0, 512), A("LF", 0, 28), A("BF", C * (lev - 6), C * (lev - 5)))
+            scan(A("KEYF", 0, 512), A("DR", 640 + 512 * (lev - 6), 1152 + 512 * (lev - 6)), A("CURF", 0, 512))
+            tr(A("TF", 0, 512), A("KEYF", 0, 512))
+            for a in range(4):
+                cp(A("TS", 0, 4, 1, 32 * a, 32 * a + 32), A("TF", 32 * a, 512, 128, 32 * a, 32 * a + 32))
+            one = lambda s: A("TS", s, s + 1)
+            if lev == 6:
+                for s in range(4):
+                    ts(A("MCF", 128 * s, 128 * s + 128), A("KEYF", 128 * s, 128 * s + 128), one(s ^ 1), OP.is_lt if s % 2 else OP.is_gt, mask("n" if s % 2 else "p"), OP.mult)
+            else:
+                for i, m in ((1, "MCG"), (0, "MCF")):
+                    ts(A(m, 0, 256), A("KEYF", 0, 256), one(2 + i), OP.is_gt, mask("p"), OP.mult)
+                    ts(A(m, 256, 512), A("KEYF", 256, 512), one(i), OP.is_lt, mask("n"), OP.mult)
+                    if i:
+                        act(A("W2", 0, C), ind(A(m, 0, 512), A("LF", 0, 28)))
+            cp(A("W1", 0, C), ind(A("MCF", 0, 512), A("LF", 0, 28)))
+            keep(lev - 1)
+            quant2("W1", "wa", "was", "wb", "wbs")
+            counts(FK, "wa", "was", "wb", "wbs", False, True, lev == 6)
+            if lev == 7:
+                quant2("W2", "ga", "gas", "gb", "gbs")
+                counts(FK, "ga", "gas", "gb", "gbs", False, False, True)
+        keep(7)
+        ts(A("RL", 0, 28), A("CK", 0, 28), 4.0, OP.mult, mask("h16"), OP.add)
+        scatter(A("SIG", 0, 480), A("RL", 0, 28), A("IOT", 0, C))
+        wrap("ZL", "SIG")
+
+        for b in range(4):
+            act(A("GZ", HALF * b, HALF * b + HALF), ind(A("HB", C * b, C * b + C), A("ZL", 0, 14)))
+        for b in range(4):
+            tt(A("ZT", b, 896, 4), ind(A("HB", C * b, C * b + C), A("ZL", 14, 28)), A("GZ", HALF * b, HALF * b + HALF), OP.add)
+        zc, zs = "zc%d" % t, "zs%d" % t
+        quant(A(zc, 0, HALF), A(zs, 0, HALF), A("ZT", 0, 896))
+
+        hazards("g", [(zc, 0, 128, 0, HALF), (zs, 0, 128, 0, HALF)], [])
+        for nm, hn, sn in ((zc, "hc%d" % t, "rc%d" % t), (zs, "hs%d" % t, "rs%d" % t)):
+            tf = []
+            for i in range(2):
+                rid, pid = topo.addr(rel[i], core)
+                s_, d_ = T[nm][:, i * HALF // 2:(i + 1) * HALF // 2], T[hn][:, :]
+                if nm == zc:
+                    s_, d_ = s_.bitcast(dt.uint8), d_.bitcast(dt.uint8)
+                tf.append(RemoteDMATransfer(dst_ids=[DstId(rid=rid, pnc=pid)], dma_engine_mask=_bits(cut[i]), remote_sem=T.sem[sn], src=s_, dst=d_))
+            g.remote_dma_fused(tf, local_sem=T.sem.snd)
+
+        ts(A("CT", 0, 28), A("CK", 0, 28), 56.0, OP.is_ge, -56.0, OP.mult)
+        tt(A("CA", 0, 28), A("CK", 0, 28), A("CT", 0, 28), OP.add)
+        ts(A("RM", 0, 28), A("CA", 0, 28), 4.0, OP.mult)
+        now = A("COL", C * t, C * t + C)
+        if t < ROUNDS - 1:
+            tt(A("KT", 0, 28), ps(FK, 0, 112, 4), A("XF", 0, 28), OP.add)
+            ts(A("R2", 0, 28), A("KT", 0, 28), 4.0, OP.mult, mask("h16"), OP.add)
+            if t == ROUNDS - 2:
+                scatter(A("OD", 0, 480), A("R2", 0, 28), now)
+                wrap("CW", "OD")
+            scatter(A("SIG", 0, 480), A("R2", 0, 28), A("IOT", 0, C))
+            wrap("PL", "SIG")
+        else:
+            scatter(A("OD", 0, 480), A("RL", 0, 28), now)
+            dmas("y", [(ext(T.od[h:h + 1, :]), A("OD", 16 * (h % 2), 16 * (h % 2) + C, 1, 16 * h, 16 * h + 1)) for h in range(8)], "dd")
+            ts(A("R2", 0, 28), A("CW", 0, 28), mask("h16"), OP.add)
+            scatter(A("SIG", 0, 480), A("R2", 0, 28), A("IOT", 0, C))
+            wrap("IC", "SIG")
+
+        lc, ls = "lc%d" % t, "ls%d" % t
+        PBANK = (0, 1, 4, 2)
+        wait("t", "lz%d" % t, landed)
+        for b in (2, 0, 3, 1):
+            mm(ps(PBANK[b], 0, HALF), A("wq", 128 * b, 128 * b + 128), A("wp", 128 * b, 128 * b + 128), A(lc, 0, HALF), A(ls, 0, HALF))
+            act(A("PB", HALF * b, HALF * b + HALF), ps(PBANK[b], 0, HALF), 0.03125)
+        for b in (2, 3):
+            act(A("RG", C * (b - 2), C * (b - 1)), ind(A("PB", HALF * b, HALF * b + HALF), A("RM", 0, 28)))
+        if t < ROUNDS - 1:
+            act(A("COL", C * t + C, C * t + 2 * C), ind(now, A("PL", 0, 28)))
+        for b in (0, 1):
+            tt(A("xn", b, 1792, 4), ind(A("PB", HALF * b, HALF * b + HALF), A("RM", 0, 28)), A("FB", C * b, C * b + C), OP.add)
+        for b in (2, 3):
+            tt(A("xn", b, 1792, 4), A("RG", C * (b - 2), C * (b - 1)), ps(DBANK[b], 0, C), OP.add)
+
+    quant(A("qx3", 0, C), A("sx3", 0, C), A("xn", 0, 1792))
+    pick("qp3", "sp3", (0, C), "qx3", "sx3", C, A("IC", 0, 28))
+    mm(ps(0, 0, C), A("qv", 0, 128), A("pv", 0, 128), A("qp3", 0, C), A("sp3", 0, C))
+    dmas("y", [(ext(T.oc[:, :]), bc(A("qp3", 0, C)))], "dc")
+    dmas("s", [(ext(T.osc[4 * k:4 * k + 4, :]), A("sp3", 0, C, 1, 32 * k, 32 * k + 4)) for k in range(4)], "dq")
+    cp(A("yb", 0, C), ps(0, 0, C))
+    dmas("y", [(ext(T.y[:, :]), A("yb", 0, C))], "dy")
+    for sem in count:
+        wait("g", sem, count[sem])
+    wait("g", "snd", 2 * len(eng) * ROUNDS)

@@ -23,14 +23,14 @@ for _n, _w in (("xt", 1792), ("xn", 1792), ("ut", 512), ("vt", 512), ("one", 576
                ("G", TW), ("WQ", TW), ("W1", TW), ("W2", TW), ("FB", 896), ("HB", 1792), ("ZT", 896), ("gm", 8)):
     _sb(_n, _w, "bfloat16")
 for _n, _w in (("MR", 384), ("MT", 384), ("KF", 28), ("KL", 8), ("BQ", 672), ("BF", 2 * C), ("CUR", 128), ("CURF", 512), ("KEY", 128),
-               ("KEYF", 512), ("TQ", 128), ("TF", 512), ("TS", 8), ("MC", 128), ("MC2", 128), ("MCF", 512), ("MCG", 512), ("TMP", 256),
+               ("KEYF", 512), ("TQ", 128), ("TF", 128), ("MC", 128), ("MC2", 128), ("MCF", 512), ("MCG", 512), ("TMP", 1024),
                ("DR", 1664), ("XL", 8), ("YL", 8), ("XK", 8), ("DK", 8), ("XF", 28), ("YF", 28), ("CK", 28), ("CT", 28), ("SIG", 480),
                ("TT", 896), ("CA", 28), ("CB", 28), ("CD", 28), ("KT", 28), ("IOT", C), ("COL", 3 * C), ("OD", 480), ("GZ", 896),
                ("PB", 896), ("RG", 2 * C), ("yb", C)):
     _sb(_n, _w)
-for _n, _w in (("pi", 28), ("ii", 84), ("ML", 8), ("MF", 28)):
+for _n, _w in (("pi", 28), ("ii", 92), ("ML", 8), ("MF", 28)):
     _sb(_n, _w, "int32")
-for _n, _w in (("LL", 8), ("LF", 28), ("RL", 28), ("RM", 28), ("R2", 28), ("ZL", 28), ("PL", 28), ("CW", 28), ("IC", 28), ("UL", 64)):
+for _n, _w in (("LL", 8), ("LF", 28), ("RL", 28), ("RM", 28), ("R2", 28), ("ZL", 28), ("PL", 28), ("CW", 28), ("IC", 28), ("UL", 72)):
     _sb(_n, _w, "uint16")
 _mx("qu", "su", 128)
 _mx("qB", "sB", 1024)
@@ -108,11 +108,11 @@ def rank_program(g, core, T, topo):
             ap = t[:, c0:c1] if (p0, p1) == (0, 128) else t[p0:p1, c0:c1]
         else:
             ap = t[:, c0:c1:st] if (p0, p1) == (0, 128) else t[p0:p1, c0:c1:st]
-        return (ap, [(name, p0, p1, c0, c1)])
+        return (ap, [(name, p0, p1, c0, c1, st)])
 
     def ps(bank, c0, c1, st=1, p0=0, p1=128):
         x = A("ps", 512 * bank + c0, 512 * bank + c1, st, p0, p1)
-        return (x[0], [("ps%d" % bank, 0, 128, 0, 512)])
+        return (x[0], [("ps%d" % bank, 0, 128, 0, 512, 1)])
 
     def ind(win, off):
         return (win[0].indirect(off[0]), win[1] + off[1])
@@ -131,10 +131,12 @@ def rank_program(g, core, T, topo):
     def hazards(q, reads, writes):
         need = {}
         for regs, w in ((reads, False), (writes, True)):
-            for (n, p0, p1, c0, c1) in regs:
+            for (n, p0, p1, c0, c1, st) in regs:
                 bank = n[:2] == "ps"
-                for (eq, sem, val, ew, a0, a1, b0, b1) in hist.get(n, ()):
+                for (eq, sem, val, ew, a0, a1, b0, b1, bs) in hist.get(n, ()):
                     if a0 >= p1 or p0 >= a1 or b0 >= c1 or c0 >= b1:
+                        continue
+                    if st == bs and (c0 - b0) % st:
                         continue
                     if bank and eq == q and (q == "t" or not ew):
                         continue
@@ -146,12 +148,13 @@ def rank_program(g, core, T, topo):
 
     def note(q, sem, val, reads, writes):
         for regs, w in ((reads, False), (writes, True)):
-            for (n, p0, p1, c0, c1) in regs:
+            for (n, p0, p1, c0, c1, st) in regs:
                 h = hist.setdefault(n, [])
                 if w:
-                    h[:] = [e for e in h if not (p0 <= e[4] and e[5] <= p1 and c0 <= e[6] and e[7] <= c1 and e[0] == q)]
-                h[:] = [e for e in h if not (e[0] == q and e[1] == sem and e[3] == w and e[4:] == (p0, p1, c0, c1))]
-                h.append((q, sem, val, w, p0, p1, c0, c1))
+                    h[:] = [e for e in h if not (p0 <= e[4] and e[5] <= p1 and c0 <= e[6] and e[7] <= c1 and e[0] == q
+                                                 and (st == 1 or (st == e[8] and (c0 - e[6]) % st == 0)))]
+                h[:] = [e for e in h if not (e[0] == q and e[1] == sem and e[3] == w and e[4:] == (p0, p1, c0, c1, st))]
+                h.append((q, sem, val, w, p0, p1, c0, c1, st))
 
     def do(q, call, outs, ins):
         reads = [r for x in ins for r in x[1]]
@@ -187,7 +190,9 @@ def rank_program(g, core, T, topo):
         do("v", lambda: g.vector.tensor_copy(out[0], a[0]), [out], [a])
 
     def act(out, a, scale=1.0):
-        if scale == 1.0:
+        if isinstance(scale, tuple):
+            do("s", lambda: g.scalar.activation(out[0], a[0], AF.Copy, scale=scale[0]), [out], [a, scale])
+        elif scale == 1.0:
             do("s", lambda: g.scalar.activation(out[0], a[0], AF.Copy), [out], [a])
         else:
             do("s", lambda: g.scalar.activation(out[0], a[0], AF.Copy, scale=scale), [out], [a])
@@ -225,24 +230,21 @@ def rank_program(g, core, T, topo):
         return (ap, [])
 
     dmas("s", [(A("pi", 0, 28, 1, 16 * h, 16 * h + 16), ext(T.p[:, :])) for h in range(0, 8)], "dp")
-    dmas("y", [(A("ut", 0, 512), ext(T.u[:, :]))], "du")
     dmas("y", [(A("xt", 0, 1792), ext(T.x[:, :]))], "dx")
+    dmas("y", [(A("ut", 0, 512), ext(T.u[:, :]))], "du")
     dmas("y", [(bc(A("wq", 0, 512)), ext(T.wc[:, :])), (A("wp", 0, 512), ext(T.ws[:, :]))], "dw")
     dmas("y", [(A("vt", 0, 512), ext(T.v[:, :]))], "dv")
 
-    for h in range(8):
-        fill(A("UL", 8 * h, 8 * h + 8), 16 * h)
     fill(A("qtr", 0, 576), 0.25)
     fill(A("one", 0, 576), 1.0)
+    for h in range(8):
+        fill(A("UL", 8 * h, 8 * h + 8), 16 * h)
     iota(A("ii", 0, 28), [[16, 28]], 0, 0)
     iota(A("ii", 28, 56), [[0, 28]], 0, 1)
+    iota(A("ii", 84, 92), [[128, 4], [16, 2]], 0, 0)
     aff(A("cb", 0, 576), A("qtr", 0, 576), [[0, 9], [1, 16], [-1, 4]], OP.is_equal, 0.0, 0, 0)
-    fill(A("CUR", 0, 128), -BIG)
-    fill(A("MC", 0, 128), 0.0)
-    fill(A("G", 0, TW), 0.0)
-    fill(A("WQ", 0, TW), 0.0)
-    quant(A("qu", 0, 128), A("su", 0, 128), A("ut", 0, 512))
-    cp(A("PL", 0, 28), A("pi", 0, 28))
+    for k in range(4):
+        act(A("cl", 512 * k, 512 * k + 512), A("one", 0, 512), 0.0)
     MASKS = {"m0": (0, 0, 1, 1.0), "lo": (1, 0, 16, 1.0), "hi": (2, 16, 32, 1.0), "h16": (3, 16, 32, 16.0),
              "b0": (4, 7, 14, 1.0), "b1": (5, 0, 7, -1.0), "b2": (6, 21, 28, 1.0), "b3": (7, 14, 21, -1.0),
              "c0": (8, 14, 28, 1.0), "c1": (9, 0, 14, -1.0), "p": (10, 0, 28, 1.0), "n": (11, 0, 28, -1.0)}
@@ -251,6 +253,9 @@ def rank_program(g, core, T, topo):
         j = MASKS[k][0]
         return A("MT", 32 * j, 32 * j + 1)
 
+    def only(a):
+        return A("MT", 0, 1, 1, 32 * a, 32 * a + 32)
+
     def phys(y, m, x):
         ts(m, x, 1.0 / 7.0, OP.mult, -27.0 / 56.0, OP.add)
         tt(y, m, x, OP.add)
@@ -258,22 +263,28 @@ def rank_program(g, core, T, topo):
     def repeat_u(h):
         pick("qB", "sB", (128 * h, 128 * h + 128), "qu", "su", 128, A("UL", 8 * h, 8 * h + 8))
 
-    def more_constants():
+    ts(A("ii", 56, 84), A("ii", 28, 56), 15, OP.bitwise_and)
+    tt(A("KF", 0, 28), A("ii", 0, 28), A("ii", 56, 84), OP.add)
+    ts(A("KF", 0, 28), A("KF", 0, 28), 0.25, OP.mult)
+    phys(A("KL", 0, 7), A("ML", 0, 7), A("KF", 0, 7))
+    tt(A("DK", 0, 7), A("KF", 0, 7), A("KL", 0, 7), OP.subtract)
+    cp(A("PL", 0, 28), A("pi", 0, 28))
+
+    def masks():
         fill(A("MR", 0, 384), 0.0)
         for k in MASKS:
             j, a, b, val = MASKS[k]
             fill(A("MR", 32 * j + a, 32 * j + b), val)
         tr(A("MT", 0, 384), A("MR", 0, 384))
-        ts(A("ii", 56, 84), A("ii", 28, 56), 15, OP.bitwise_and)
-        tt(A("KF", 0, 28), A("ii", 0, 28), A("ii", 56, 84), OP.add)
-        ts(A("KF", 0, 28), A("KF", 0, 28), 0.25, OP.mult)
-        phys(A("KL", 0, 7), A("ML", 0, 7), A("KF", 0, 7))
-        tt(A("DK", 0, 7), A("KF", 0, 7), A("KL", 0, 7), OP.subtract)
-        fill(A("cl", 0, 2048), 0.0)
+
+    def more_constants():
         for k in range(4):
             s = 4 * ((16 - 4 * k) % 16)
             for a in range(4):
-                cp(A("cl", 512 * k + 128 * a, 512 * k + 128 * a + 128, 1, 32 * a, 32 * a + 32), A("cb", s + 128 * a, s + 128 * a + 128, 1, 32 * a, 32 * a + 32))
+                act(A("cl", 512 * k + 128 * a, 512 * k + 128 * a + 128, 1, 32 * a, 32 * a + 32), A("cb", s + 128 * a, s + 128 * a + 128, 1, 32 * a, 32 * a + 32))
+        fill(A("G", 0, TW), 0.0)
+        fill(A("WQ", 0, TW), 0.0)
+        quant(A("qcb", 0, 144), A("scb", 0, 144), A("cb", 0, 576))
 
     def never(name, a, b, val):
         aff(A(name, a, b), A("IOT", 0, b - a), [[0, b - a]], OP.is_equal, val, 1, 0)
@@ -282,6 +293,7 @@ def rank_program(g, core, T, topo):
     never("DR", 0, 320, BIG)
     never("DR", 320, 640, BIG)
     aff(A("gm", 0, 8), A("one", 0, 8), [[-16, 8]], OP.is_ge, 0.0, 0, 1)
+    aff(A("gm", 0, 1), A("one", 0, 1), [[0, 1]], OP.is_ge, 0.0, 15, -1)
     aff(A("eb", 0, 516), A("one", 0, 516), [[1, 516]], OP.is_equal, 0.0, -3, -4)
     for c0 in (640, 984, 1328):
         never("DR", c0, min(c0 + 344, 1664), BIG)
@@ -297,7 +309,6 @@ def rank_program(g, core, T, topo):
             fill(A("DR", 640, 1152, 128), -BIG)
             fill(A("DR", 1152, 1664, 256), -BIG)
             return
-        fill(A("DR", 0, 128, 2), -BIG)
         for s in (0, 7, 14, 21):
             fill(A("DR", 128 + s, 256, 32), -BIG)
         for s in (0, 14):
@@ -319,9 +330,12 @@ def rank_program(g, core, T, topo):
         quant(A(ca, 0, 132), A(cas, 0, 132), A(tile, 0, 528))
         quant(A(cb_, 0, 132), A(cbs, 0, 132), A(tile, 4, 532))
 
-    def wrap(dst, row):
-        tr(A("TT", 0, C), A(row, 0, C))
-        tr(A("TT", C, 2 * C), A(row, 16, 16 + C))
+    def wrap(dst, row, part=2):
+        if part != 1:
+            tr(A("TT", 0, C), A(row, 0, C))
+            tr(A("TT", C, 2 * C), A(row, 16, 16 + C))
+        if part == 0:
+            return
         ts(A("CA", 0, 28), A("TT", 0, 896, 32), mask("lo"), OP.mult)
         ts(A("CB", 0, 28), A("TT", 16, 896, 32), mask("hi"), OP.mult)
         tt(A("CD", 0, 28), A("CA", 0, 28), A("CB", 0, 28), OP.add)
@@ -330,6 +344,7 @@ def rank_program(g, core, T, topo):
 
     SBANK = [0, 1, 2, 3, 6, 7, 0, 1]
     DBANK = [2, 3, 6, 7]
+    PBANK = [0, 1, 4, 2]
     dst = T.cores[(rank + 1) % len(T.cores)]
     rel = _relays(topo, core, dst)
     eng = topo.engines(core, rel[0])
@@ -342,13 +357,23 @@ def rank_program(g, core, T, topo):
         for i in range(2):
             pick(qp, sp, (HALF * i, HALF * i + HALF), qx, sx, C, A("PL", 14 * i, 14 * i + 14))
         if t == 0:
-            repeat_u(0)
-        for i, bank in enumerate((0, 4)):
-            o = (HALF * i, HALF * i + HALF)
-            mm(ps(bank, 0, HALF), A("qB", 0, 128), A("sB", 0, 128), A(qp, *o), A(sp, *o))
-            for a in (2 * i, 2 * i + 1):
-                out, in_ = A("BQ", 0, 112, 1, 32 * a, 32 * a + 32), ps(bank, 112 * (a % 2), 112 * (a % 2) + 112, 1, 32 * a, 32 * a + 32)
-                (act if i == 0 else cp)(out, in_)
+            quant(A("qu", 0, 128), A("su", 0, 128), A("ut", 0, 512))
+        for h in range(2):
+            if t == 0:
+                repeat_u(h)
+            for i, bank in enumerate(((0, 4), (1, 5))[h]):
+                o = (HALF * i, HALF * i + HALF)
+                mm(ps(bank, 0, HALF), A("qB", 128 * h, 128 * h + 128), A("sB", 128 * h, 128 * h + 128), A(qp, *o), A(sp, *o))
+        if t == 0:
+            masks()
+        for h in range(2):
+            for i, bank in enumerate(((0, 4), (1, 5))[h]):
+                for a in (2 * i, 2 * i + 1):
+                    out, in_ = A("BQ", 112 * h, 112 * h + 112, 1, 32 * a, 32 * a + 32), ps(bank, 112 * (a % 2), 112 * (a % 2) + 112, 1, 32 * a, 32 * a + 32)
+                    if i == 0:
+                        act(out, in_, only(a))
+                    else:
+                        ts(out, in_, only(a), OP.mult)
 
         def scores(h):
             mm(ps(SBANK[h], 0, C), A("qB", 128 * h, 128 * h + 128), A("sB", 128 * h, 128 * h + 128), A(qp, 0, C), A(sp, 0, C))
@@ -368,19 +393,12 @@ def rank_program(g, core, T, topo):
 
         if t == 0:
             more_constants()
-            repeat_u(1)
-        ts(A("LL", 0, 7), A("KL", 0, 7), 4.0, OP.mult)
-        if t == 0:
-            quant(A("qcb", 0, 144), A("scb", 0, 144), A("cb", 0, 576))
-            for k in range(4):
-                quant(A("qcl", 128 * k, 128 * k + 128), A("scl", 128 * k, 128 * k + 128), A("cl", 512 * k, 512 * k + 512))
-        scores(1)
-        evac(1)
+            repeat_u(2)
+        scores(2)
+        evac(2)
 
         def background(lev):
             if t == 0:
-                if lev == 0:
-                    resets(False)
                 if lev < 6:
                     repeat_u(lev + 2)
                 if lev == 1:
@@ -389,6 +407,10 @@ def rank_program(g, core, T, topo):
                     act(A("COL", 0, C), ind(A("IOT", 0, C), A("PL", 0, 28)))
                 if lev == 5:
                     resets(True)
+                    ts(A("ii", 0, 8), A("ii", 28, 36), 96, OP.bitwise_and)
+                    tt(A("ii", 0, 8), A("ii", 0, 8), A("ii", 84, 92), OP.add)
+                    tt(A("ii", 0, 8), A("ii", 0, 8), A("ii", 56, 64), OP.add)
+                    cp(A("UL", 64, 72), A("ii", 0, 8))
                     quant(A("qv", 0, 128), A("pv", 0, 128), A("vt", 0, 512))
             scores(lev + 2)
             evac(lev + 2)
@@ -399,63 +421,96 @@ def rank_program(g, core, T, topo):
         def keep(lev):
             f = ps(FK, 0, 112, 4)
             ts(A("CT", 0, 28), f, A("gm", lev, lev + 1), OP.mult)
-            if lev < 5:
-                tt(A("XF", 0, 28), f, A("XF" if lev else "KF", 0, 28), OP.add)
+            if 0 < lev < 5:
+                tt(A("XF", 0, 28), f, A("XF" if lev > 1 else "KF", 0, 28), OP.add)
             tt(A("CK", 0, 28), A("CK" if lev else "KF", 0, 28), A("CT", 0, 28), OP.add)
 
-        for lev in range(6):
+        def spread(src, lev, c0=0):
+            for a in range(4):
+                (cp if a < 2 or lev in (0, 5) else act)(A("WQ", 112 * a, 112 * a + 112, 1, 32 * a, 32 * a + 32), A(src, c0, c0 + 112, 1, 32 * a, 32 * a + 32))
+
+        V = lambda n: A("TMP", 56 * n, 56 * n + 56)
+        L = lambda n: A("TMP", 56 * n, 56 * n + 56, 2)
+        R = lambda n: A("TMP", 56 * n + 1, 56 * n + 56, 2)
+        H = lambda n: A("TMP", 28 * n, 28 * n + 28)
+        s0, s1 = [[A("BQ", 112 * h + i, 112 * h + 112, 2) for i in range(2)] for h in range(2)]
+        tt(V(0), s0[1], s0[0], OP.is_lt)
+        tt(V(1), s1[0], s1[1], OP.max)
+        ts(V(2), V(0), -2 * BIG, OP.mult, BIG, OP.add)
+        ts(V(3), V(0), 2 * BIG, OP.mult, -BIG, OP.add)
+        cp(A("G", 256, 368, 2), V(0))
+        ts(A("G", 257, 368, 2), V(0), -1.0, OP.mult)
+        tt(V(2), s1[0], V(2), OP.min)
+        tt(V(3), s1[1], V(3), OP.min)
+        if t == 0:
+            fill(A("CUR", 0, 128), -BIG)
+            fill(A("MC", 0, 128), 0.0)
+        tt(V(4), V(2), V(3), OP.max)
+        if t == 0:
+            resets(False)
+        tt(H(10), L(4), R(4), OP.is_gt)
+        tt(H(11), L(4), R(1), OP.is_gt)
+        tt(H(12), L(1), R(4), OP.is_gt)
+        tt(H(13), L(1), R(1), OP.is_gt)
+        tt(H(14), H(10), H(11), OP.add)
+        tt(H(15), H(12), H(13), OP.add)
+        tt(H(16), H(10), H(12), OP.add)
+        tt(H(17), H(11), H(13), OP.add)
+        tt(H(18), H(15), H(14), OP.subtract)
+        tt(H(19), H(17), H(16), OP.subtract)
+        tt(H(20), H(14), L(0), OP.add)
+        tt(H(21), H(15), L(0), OP.subtract)
+        tt(H(22), R(0), H(16), OP.subtract)
+        tt(H(23), H(17), R(0), OP.add)
+        tt(H(18), H(18), L(0), OP.mult)
+        tt(H(19), H(19), R(0), OP.mult)
+        tt(A("G", 0, 112, 4), H(20), H(18), OP.add)
+        tt(A("G", 1, 112, 4), H(21), H(18), OP.subtract)
+        tt(A("G", 2, 112, 4), H(22), H(19), OP.subtract)
+        tt(A("G", 3, 112, 4), H(19), H(23), OP.subtract)
+        if t == 0:
+            for k in range(4):
+                quant(A("qcl", 128 * k, 128 * k + 128), A("scl", 128 * k, 128 * k + 128), A("cl", 512 * k, 512 * k + 512))
+        quant2("G", "ga", "gas", "gb", "gbs")
+        counts(LB, "ga", "gas", "gb", "gbs", True)
+        spread("G", 0, 256)
+        quant2("WQ", "wa", "was", "wb", "wbs")
+        counts(FK, "wa", "was", "wb", "wbs", False)
+        spread("G", 0)
+        tt(A("XL", 0, 7), ps(LB, 0, 28, 4), A("KL", 0, 7), OP.add)
+        ts(A("LL", 0, 7), A("XL", 0, 7), 4.0, OP.mult)
+        background(1)
+
+        for lev in range(2, 6):
             scatter(A("CUR", 0, 128), A("LL", 0, 7), A("BQ", 112 * lev, 112 * lev + 112))
-            first = None
-            if lev == 0:
-                tt(A("MC", 0, 128, 2), A("CUR", 1, 128, 2), A("CUR", 0, 128, 2), OP.is_lt)
-                ts(A("MC", 1, 128, 2), A("MC", 0, 128, 2), -1.0, OP.mult)
-                first = mask("m0")
+            if lev == 2:
+                keep(0)
+                quant2("WQ", "wa", "was", "wb", "wbs")
+                counts(FK, "wa", "was", "wb", "wbs", False)
+            scan(A("KEY", 0, 128), A("DR", 128 * (lev - 1), 128 * lev), A("CUR", 0, 128))
+            tr(A("TQ", 0, 128), A("KEY", 0, 128))
+            one = lambda b: A("TQ", 32 * b, 32 * b + 1)
+            if lev in (2, 3):
+                w = BLK[lev]
+                for b in range(4):
+                    for j in range(28 // w):
+                        a = 32 * b + w * j
+                        ts(A("MC", a, a + w), A("KEY", a, a + w), one(b), OP.is_lt if j % 2 else OP.is_gt, mask(("b%d" if lev == 2 else "c%d") % j), OP.mult)
+            elif lev == 4:
+                for b in range(4):
+                    a = 32 * b
+                    ts(A("MC", a, a + 32), A("KEY", a, a + 32), one(b ^ 1), OP.is_lt if b % 2 else OP.is_gt, mask("n" if b % 2 else "p"), OP.mult)
             else:
-                scan(A("KEY", 0, 128), A("DR", 128 * (lev - 1), 128 * lev), A("CUR", 0, 128))
-            if lev == 1:
-                k = [A("KEY", i, 128, 4) for i in range(4)]
-                c = [A("TMP", 32 * i, 32 * i + 32) for i in range(4)]
-                tt(c[0], k[0], k[2], OP.is_gt)
-                tt(c[1], k[0], k[3], OP.is_gt)
-                tt(c[2], k[1], k[2], OP.is_gt)
-                tt(c[3], k[1], k[3], OP.is_gt)
-                ts(A("TMP", 128, 256), A("TMP", 0, 128), -1.0, OP.mult)
-                tt(A("MC", 0, 128, 4), c[0], c[1], OP.add)
-                tt(A("MC", 1, 128, 4), c[2], c[3], OP.add)
-                n = [A("TMP", 128 + 32 * i, 160 + 32 * i) for i in range(4)]
-                tt(A("MC", 2, 128, 4), n[0], n[2], OP.add)
-                tt(A("MC", 3, 128, 4), n[1], n[3], OP.add)
-                first = mask("m0")
-            if lev > 1:
-                tr(A("TQ", 0, 128), A("KEY", 0, 128))
-                one = lambda b: A("TQ", 32 * b, 32 * b + 1)
-                if lev in (2, 3):
-                    w = BLK[lev]
-                    for b in range(4):
-                        for j in range(28 // w):
-                            a = 32 * b + w * j
-                            ts(A("MC", a, a + w), A("KEY", a, a + w), one(b), OP.is_lt if j % 2 else OP.is_gt, mask(("b%d" if lev == 2 else "c%d") % j), OP.mult)
-                elif lev == 4:
-                    for b in range(4):
-                        a = 32 * b
-                        ts(A("MC", a, a + 32), A("KEY", a, a + 32), one(b ^ 1), OP.is_lt if b % 2 else OP.is_gt, mask("n" if b % 2 else "p"), OP.mult)
-                else:
-                    for i, m in enumerate(("MC", "MC2")):
-                        ts(A(m, 0, 64), A("KEY", 0, 64), one(2 + i), OP.is_gt, mask("p"), OP.mult)
-                        ts(A(m, 64, 128), A("KEY", 64, 128), one(i), OP.is_lt, mask("n"), OP.mult)
-                    tt(A("MC", 0, 128), A("MC", 0, 128), A("MC2", 0, 128), OP.add)
-            back = ind(A("MC", 0, 128), A("LL", 0, 7))
-            if first is not None:
-                ts(A("G", 0, 112), back, first, OP.mult)
-            else:
-                cp(A("G", 0, 112), back)
+                for i, m in enumerate(("MC", "MC2")):
+                    ts(A(m, 0, 64), A("KEY", 0, 64), one(2 + i), OP.is_gt, mask("p"), OP.mult)
+                    ts(A(m, 64, 128), A("KEY", 64, 128), one(i), OP.is_lt, mask("n"), OP.mult)
+                tt(A("MC", 0, 128), A("MC", 0, 128), A("MC2", 0, 128), OP.add)
+            cp(A("G", 0, 112), ind(A("MC", 0, 128), A("LL", 0, 7)))
             if lev < 5:
                 quant2("G", "ga", "gas", "gb", "gbs")
                 counts(LB, "ga", "gas", "gb", "gbs", True)
-            for a in range(4):
-                (cp if a < 2 or lev == 5 else act)(A("WQ", 112 * a, 112 * a + 112, 1, 32 * a, 32 * a + 32), A("G", 0, 112, 1, 32 * a, 32 * a + 32))
-            if lev > 0:
-                keep(lev - 1)
+            spread("G", lev)
+            keep(lev - 1)
             if lev == 4:
                 tt(A("XK", 0, 7), A("XL", 0, 7), A("DK", 0, 7), OP.add)
             quant2("WQ", "wa", "was", "wb", "wbs")
@@ -463,7 +518,7 @@ def rank_program(g, core, T, topo):
             if lev < 5:
                 loc = ps(LB, 0, 28, 4)
                 if lev < 4:
-                    tt(A("XL", 0, 7), loc, A("XL" if lev else "KL", 0, 7), OP.add)
+                    tt(A("XL", 0, 7), loc, A("XL", 0, 7), OP.add)
                     ts(A("LL", 0, 7), A("XL", 0, 7), 4.0, OP.mult)
                 else:
                     tt(A("XL", 0, 7), loc, A("XK", 0, 7), OP.add)
@@ -471,16 +526,17 @@ def rank_program(g, core, T, topo):
                     ts(A("LL", 0, 7), A("YL", 0, 7), 4.0, OP.mult)
             background(lev)
 
+        if t == ROUNDS - 1:
+            scatter(A("OD", 0, 480), A("R2", 0, 28), A("COL", C * t - C, C * t))
         for lev in (6, 7):
             tt(A("XF", 0, 28), ps(FK, 0, 112, 4), A("XF", 0, 28), OP.add)
             phys(A("YF", 0, 28), A("MF", 0, 28), A("XF", 0, 28))
             ts(A("LF", 0, 28), A("YF", 0, 28), 4.0, OP.mult)
             scatter(A("CURF", 0, 512), A("LF", 0, 28), A("BF", C * (lev - 6), C * (lev - 5)))
             scan(A("KEYF", 0, 512), A("DR", 640 + 512 * (lev - 6), 1152 + 512 * (lev - 6)), A("CURF", 0, 512))
-            tr(A("TF", 0, 512), A("KEYF", 0, 512))
-            for a in range(4):
-                cp(A("TS", 0, 4, 1, 32 * a, 32 * a + 32), A("TF", 32 * a, 512, 128, 32 * a, 32 * a + 32))
-            one = lambda s: A("TS", s, s + 1)
+            cp(A("TMP", 0, 128), ind(A("KEYF", 0, 512), A("UL", 64, 72)))
+            tr(A("TF", 0, 128), A("TMP", 0, 128))
+            one = lambda s: A("TF", 32 * s, 32 * s + 1)
             if lev == 6:
                 for s in range(4):
                     ts(A("MCF", 128 * s, 128 * s + 128), A("KEYF", 128 * s, 128 * s + 128), one(s ^ 1), OP.is_lt if s % 2 else OP.is_gt, mask("n" if s % 2 else "p"), OP.mult)
@@ -497,19 +553,21 @@ def rank_program(g, core, T, topo):
             if lev == 7:
                 quant2("W2", "ga", "gas", "gb", "gbs")
                 counts(FK, "ga", "gas", "gb", "gbs", False, False, True)
+            if t == ROUNDS - 1:
+                wrap("CW", "OD", lev - 6)
         keep(7)
         ts(A("RL", 0, 28), A("CK", 0, 28), 4.0, OP.mult, mask("h16"), OP.add)
         scatter(A("SIG", 0, 480), A("RL", 0, 28), A("IOT", 0, C))
         wrap("ZL", "SIG")
 
         for b in range(4):
-            act(A("GZ", HALF * b, HALF * b + HALF), ind(A("HB", C * b, C * b + C), A("ZL", 0, 14)))
+            (act if b else cp)(A("GZ", HALF * b, HALF * b + HALF), ind(A("HB", C * b, C * b + C), A("ZL", 0, 14)))
         for b in range(4):
             tt(A("ZT", b, 896, 4), ind(A("HB", C * b, C * b + C), A("ZL", 14, 28)), A("GZ", HALF * b, HALF * b + HALF), OP.add)
         zc, zs = "zc%d" % t, "zs%d" % t
         quant(A(zc, 0, HALF), A(zs, 0, HALF), A("ZT", 0, 896))
 
-        hazards("g", [(zc, 0, 128, 0, HALF), (zs, 0, 128, 0, HALF)], [])
+        hazards("g", [(zc, 0, 128, 0, HALF, 1), (zs, 0, 128, 0, HALF, 1)], [])
         for nm, hn, sn in ((zc, "hc%d" % t, "rc%d" % t), (zs, "hs%d" % t, "rs%d" % t)):
             tf = []
             for i in range(2):
@@ -527,20 +585,14 @@ def rank_program(g, core, T, topo):
         if t < ROUNDS - 1:
             tt(A("KT", 0, 28), ps(FK, 0, 112, 4), A("XF", 0, 28), OP.add)
             ts(A("R2", 0, 28), A("KT", 0, 28), 4.0, OP.mult, mask("h16"), OP.add)
-            if t == ROUNDS - 2:
-                scatter(A("OD", 0, 480), A("R2", 0, 28), now)
-                wrap("CW", "OD")
             scatter(A("SIG", 0, 480), A("R2", 0, 28), A("IOT", 0, C))
             wrap("PL", "SIG")
         else:
-            scatter(A("OD", 0, 480), A("RL", 0, 28), now)
-            dmas("y", [(ext(T.od[h:h + 1, :]), A("OD", 16 * (h % 2), 16 * (h % 2) + C, 1, 16 * h, 16 * h + 1)) for h in range(8)], "dd")
             ts(A("R2", 0, 28), A("CW", 0, 28), mask("h16"), OP.add)
             scatter(A("SIG", 0, 480), A("R2", 0, 28), A("IOT", 0, C))
             wrap("IC", "SIG")
 
         lc, ls = "lc%d" % t, "ls%d" % t
-        PBANK = (0, 1, 4, 2)
         wait("t", "lz%d" % t, landed)
         for b in (2, 0, 3, 1):
             mm(ps(PBANK[b], 0, HALF), A("wq", 128 * b, 128 * b + 128), A("wp", 128 * b, 128 * b + 128), A(lc, 0, HALF), A(ls, 0, HALF))
@@ -561,6 +613,8 @@ def rank_program(g, core, T, topo):
     dmas("s", [(ext(T.osc[4 * k:4 * k + 4, :]), A("sp3", 0, C, 1, 32 * k, 32 * k + 4)) for k in range(4)], "dq")
     cp(A("yb", 0, C), ps(0, 0, C))
     dmas("y", [(ext(T.y[:, :]), A("yb", 0, C))], "dy")
+    scatter(A("OD", 0, 480), A("RL", 0, 28), A("COL", C * t, C * t + C))
+    dmas("s", [(ext(T.od[h:h + 1, :]), A("OD", 16 * (h % 2), 16 * (h % 2) + C, 1, 16 * h, 16 * h + 1)) for h in range(8)], "dd")
     for sem in count:
         wait("g", sem, count[sem])
     wait("g", "snd", 2 * len(eng) * ROUNDS)

from concourse.bass import DstId, RemoteDMATransfer
from concourse.mybir import dt, AluOpType, ActivationFunctionType

OP = AluOpType
AF = ActivationFunctionType
ROUNDS, C, HALF = 3, 448, 224
BIG = 1e29
TW = 536

SCRATCH = {}


def _sb(name, n, ty="float32"):
    SCRATCH[name] = ("sbuf", [128, n], ty)


def _mx(c, s, n):
    _sb(c, n, "float8_e4m3fn_x4")
    _sb(s, n, "uint8")


for _n, _w in (("xt", 1792), ("xn", 1792), ("ut", 512), ("vt", 512), ("one", 576), ("qtr", 576), ("eb", 516), ("cb", 576), ("cl", 2048),
               ("G", TW), ("WQ", TW), ("W1", TW), ("W2", TW), ("FB", 896), ("HB", 1792), ("ZT", 896), ("gm", 8)):
    _sb(_n, _w, "bfloat16")
for _n, _w in (("MR", 384), ("MT", 384), ("KF", 28), ("KL", 8), ("BQ", 672), ("BF", 2 * C), ("CUR", 128), ("CURF", 512), ("KEY", 128),
               ("KEYF", 512), ("TQ", 128), ("TF", 128), ("MC", 128), ("MC2", 128), ("MCF", 512), ("MCG", 512), ("TMP", 1024),
               ("DR", 1664), ("XL", 8), ("YL", 8), ("XK", 8), ("DK", 8), ("XF", 28), ("YF", 28), ("CK", 28), ("CT", 28), ("SIG", 480),
               ("TT", 896), ("CA", 28), ("CB", 28), ("CD", 28), ("KT", 28), ("IOT", C), ("COL", 3 * C), ("OD", 480), ("GZ", 896),
               ("PB", 896), ("RG", 2 * C), ("yb", C)):
    _sb(_n, _w)
for _n, _w in (("pi", 28), ("ii", 92), ("ML", 8), ("MF", 28)):
    _sb(_n, _w, "int32")
for _n, _w in (("LL", 8), ("LF", 28), ("RL", 28), ("RM", 28), ("R2", 28), ("ZL", 28), ("PL", 28), ("CW", 28), ("IC", 28), ("UL", 72)):
    _sb(_n, _w, "uint16")
_mx("qu", "su", 128)
_mx("qB", "sB", 1024)
_mx("qv", "pv", 128)
_mx("wq", "wp", 512)
_mx("qcb", "scb", 144)
_mx("qcl", "scl", 512)
_mx("qe", "se", 512)
_mx("ga", "gas", 132)
_mx("gb", "gbs", 132)
_mx("wa", "was", 132)
_mx("wb", "wbs", 132)
for _t in range(ROUNDS + 1):
    _mx("qx%d" % _t, "sx%d" % _t, C)
    _mx("qp%d" % _t, "sp%d" % _t, C)
for _t in range(ROUNDS):
    _mx("zc%d" % _t, "zs%d" % _t, HALF)
    _mx("lc%d" % _t, "ls%d" % _t, HALF)
    _mx("hc%d" % _t, "hs%d" % _t, HALF // 2)
SCRATCH["ps"] = ("psum", [128, 4096], "float32")

SEMAPHORES = (["sv", "st", "ss", "sg", "snd", "dx", "dp", "du", "dw", "dv", "dy", "dc", "dd", "dq"]
              + ["%s%d" % (_a, _t) for _a in ("rc", "rs", "lz") for _t in range(ROUNDS)])


def _relays(topo, src, dst):
    ok = [c for c in topo.cores_of(src) if c != src and topo.may_write(c, dst)]
    near = [c for c in ok if topo.die(c) == topo.die(src)]
    far = [c for c in ok if topo.die(c) != topo.die(src)]
    return [near[0], far[0]]


def _bits(engines):
    m = 0
    for e in engines:
        m |= 1 << e
    return m


def _relay_program(g, core, T, topo):
    n = len(T.cores)
    for r in range(n):
        dst = T.cores[(r + 1) % n]
        rel = _relays(topo, T.cores[r], dst)
        if core not in rel:
            continue
        h = rel.index(core)
        a, b = h * HALF // 2, (h + 1) * HALF // 2
        rid, pid = topo.addr(dst, core)
        m = topo.mask(core, dst)
        k = len(topo.engines(core, dst))
        half = len(topo.engines(T.cores[r], core)) // 2
        for t in range(ROUNDS):
            g.wait_ge(T.sem["rc%d" % t], half)
            g.remote_dma(T["lc%d" % t][:, a:b].bitcast(dt.uint8), T["hc%d" % t][:, :].bitcast(dt.uint8), T.sem["lz%d" % t], T.sem.snd, pid, rid, m)
            g.wait_ge(T.sem["rs%d" % t], half)
            g.remote_dma(T["ls%d" % t][:, a:b], T["hs%d" % t][:, :], T.sem["lz%d" % t], T.sem.snd, pid, rid, m)
        g.wait_ge(T.sem.snd, 2 * k * ROUNDS)


def rank_program(g, core, T, topo):
    rank = T.rank_of(core)
    if rank is None:
        _relay_program(g, core, T, topo)
        return
    Q = {"v": g.vector, "t": g.tensor, "s": g.scalar, "g": g, "y": g.sync}
    ESEM = {"v": "sv", "t": "st", "s": "ss", "g": "sg"}
    count = {"sv": 0, "st": 0, "ss": 0, "sg": 0}
    seen = {}
    hist = {}

    def A(name, c0, c1, st=1, p0=0, p1=128):
        t = T[name]
        if st == 1:
            ap = t[:, c0:c1] if (p0, p1) == (0, 128) else t[p0:p1, c0:c1]
        else:
            ap = t[:, c0:c1:st] if (p0, p1) == (0, 128) else t[p0:p1, c0:c1:st]
        return (ap, [(name, p0, p1, c0, c1, st)])

    def ps(bank, c0, c1, st=1, p0=0, p1=128):
        x = A("ps", 512 * bank + c0, 512 * bank + c1, st, p0, p1)
        return (x[0], [("ps%d" % bank, 0, 128, 0, 512, 1)])

    def ind(win, off):
        return (win[0].indirect(off[0]), win[1] + off[1])

    def bc(x):
        return (x[0].bitcast(dt.uint8), x[1])

    def u32(x):
        return (x[0].bitcast(dt.uint32), x[1])

    def wait(q, sem, val):
        if seen.get((q, sem), 0) < val:
            Q[q].wait_ge(T.sem[sem], val)
            seen[(q, sem)] = val

    def hazards(q, reads, writes):
        need = {}
        for regs, w in ((reads, False), (writes, True)):
            for (n, p0, p1, c0, c1, st) in regs:
                bank = n[:2] == "ps"
                for (eq, sem, val, ew, a0, a1, b0, b1, bs) in hist.get(n, ()):
                    if a0 >= p1 or p0 >= a1 or b0 >= c1 or c0 >= b1:
                        continue
                    if st == bs and (c0 - b0) % st:
                        continue
                    if bank and eq == q and (q == "t" or not ew):
                        continue
                    if not bank and not w and not ew:
                        continue
                    need[sem] = max(need.get(sem, 0), val)
        for sem in need:
            wait(q, sem, need[sem])

    def note(q, sem, val, reads, writes):
        for regs, w in ((reads, False), (writes, True)):
            for (n, p0, p1, c0, c1, st) in regs:
                h = hist.setdefault(n, [])
                if w:
                    h[:] = [e for e in h if not (p0 <= e[4] and e[5] <= p1 and c0 <= e[6] and e[7] <= c1 and e[0] == q
                                                 and (st == 1 or (st == e[8] and (c0 - e[6]) % st == 0)))]
                h[:] = [e for e in h if not (e[0] == q and e[1] == sem and e[3] == w and e[4:] == (p0, p1, c0, c1, st))]
                h.append((q, sem, val, w, p0, p1, c0, c1, st))

    def do(q, call, outs, ins):
        reads = [r for x in ins for r in x[1]]
        writes = [r for x in outs for r in x[1]]
        hazards(q, reads, writes)
        sem = ESEM[q]
        count[sem] += 1
        call().then_inc(T.sem[sem], 1)
        note(q, sem, count[sem], reads, writes)

    def dmas(q, pairs, sem):
        for out, in_ in pairs:
            hazards(q, in_[1], out[1])
        for out, in_ in pairs:
            Q[q].dma_start(out[0], in_[0]).then_inc(T.sem[sem], 16)
        count[sem] = count.get(sem, 0) + 16 * len(pairs)
        for out, in_ in pairs:
            note("d" + sem, sem, count[sem], in_[1], out[1])

    def tt(out, a, b, op):
        do("v", lambda: g.vector.tensor_tensor(out[0], a[0], b[0], op), [out], [a, b])

    def ts(out, a, s1, op0, s2=None, op1=None):
        ins = [a] + [x for x in (s1, s2) if isinstance(x, tuple)]
        v1 = s1[0] if isinstance(s1, tuple) else s1
        v2 = s2[0] if isinstance(s2, tuple) else s2
        if op1 is None:
            do("v", lambda: g.vector.tensor_scalar(out[0], a[0], v1, None, op0), [out], ins)
        else:
            do("v", lambda: g.vector.tensor_scalar(out[0], a[0], v1, v2, op0, op1), [out], ins)

    def cp(out, a):
        do("v", lambda: g.vector.tensor_copy(out[0], a[0]), [out], [a])

    def act(out, a, scale=1.0):
        if isinstance(scale, tuple):
            do("s", lambda: g.scalar.activation(out[0], a[0], AF.Copy, scale=scale[0]), [out], [a, scale])
        elif scale == 1.0:
            do("s", lambda: g.scalar.activation(out[0], a[0], AF.Copy), [out], [a])
        else:
            do("s", lambda: g.scalar.activation(out[0], a[0], AF.Copy, scale=scale), [out], [a])

    def pick(qo, so, o, qi, si, w, off):
        act(A(so, *o), ind(A(si, 0, w), off))
        src = A(qi, 0, w)
        do("v", lambda: g.vector.tensor_copy(u32(A(qo, *o))[0], u32(src)[0].indirect(off[0])), [A(qo, *o)], [src, off])

    def scatter(win, off, vals):
        do("v", lambda: g.vector.tensor_copy(win[0].indirect(off[0]), vals[0]), [win], [vals, off])

    def scan(out, d0, d1):
        do("v", lambda: g.vector.tensor_tensor_scan(out[0], d0[0], d1[0], -BIG, OP.min, OP.max), [out], [d0, d1])

    def tr(out, a):
        do("v", lambda: g.vector.transpose(out[0], a[0]), [out], [a])

    def fill(x, val):
        do("v", lambda: g.vector.memset(x[0], val), [x], [])

    def quant(c, s, a):
        do("v", lambda: g.vector.quantize_mx(c[0], s[0], a[0]), [c, s], [a])

    def mm(out, w, ws, x, xs, start=True, stop=True):
        do("t", lambda: g.tensor.matmul_mx(out[0], w[0], ws[0], x[0], xs[0], start, stop), [out], [w, ws, x, xs])

    def aff(out, in_, pattern, op, val, base, cm):
        do("g", lambda: g.affine_select(out[0], in_[0], pattern, op, val, base, cm), [out], [in_])

    def iota(out, pattern, base, cm):
        do("g", lambda: g.iota(out[0], pattern, base, cm, allow_small_or_imprecise_dtypes=True), [out], [])

    def ext(ap):
        return (ap, [])

    dmas("s", [(A("pi", 0, 28, 1, 16 * h, 16 * h + 16), ext(T.p[:, :])) for h in range(0, 8)], "dp")
    dmas("y", [(A("xt", 0, 1792), ext(T.x[:, :]))], "dx")
    dmas("y", [(A("ut", 0, 512), ext(T.u[:, :]))], "du")
    dmas("y", [(bc(A("wq", 0, 512)), ext(T.wc[:, :])), (A("wp", 0, 512), ext(T.ws[:, :]))], "dw")
    dmas("y", [(A("vt", 0, 512), ext(T.v[:, :]))], "dv")

    fill(A("qtr", 0, 576), 0.25)
    fill(A("one", 0, 576), 1.0)
    for h in range(8):
        fill(A("UL", 8 * h, 8 * h + 8), 16 * h)
    iota(A("ii", 0, 28), [[16, 28]], 0, 0)
    iota(A("ii", 28, 56), [[0, 28]], 0, 1)
    iota(A("ii", 84, 92), [[128, 4], [16, 2]], 0, 0)
    aff(A("cb", 0, 576), A("qtr", 0, 576), [[0, 9], [1, 16], [-1, 4]], OP.is_equal, 0.0, 0, 0)
    for k in range(4):
        act(A("cl", 512 * k, 512 * k + 512), A("one", 0, 512), 0.0)
    MASKS = {"m0": (0, 0, 1, 1.0), "lo": (1, 0, 16, 1.0), "hi": (2, 16, 32, 1.0), "h16": (3, 16, 32, 16.0),
             "b0": (4, 7, 14, 1.0), "b1": (5, 0, 7, -1.0), "b2": (6, 21, 28, 1.0), "b3": (7, 14, 21, -1.0),
             "c0": (8, 14, 28, 1.0), "c1": (9, 0, 14, -1.0), "p": (10, 0, 28, 1.0), "n": (11, 0, 28, -1.0)}

    def mask(k):
        j = MASKS[k][0]
        return A("MT", 32 * j, 32 * j + 1)

    def only(a):
        return A("MT", 0, 1, 1, 32 * a, 32 * a + 32)

    def phys(y, m, x):
        ts(m, x, 1.0 / 7.0, OP.mult, -27.0 / 56.0, OP.add)
        tt(y, m, x, OP.add)

    def repeat_u(h):
        pick("qB", "sB", (128 * h, 128 * h + 128), "qu", "su", 128, A("UL", 8 * h, 8 * h + 8))

    ts(A("ii", 56, 84), A("ii", 28, 56), 15, OP.bitwise_and)
    tt(A("KF", 0, 28), A("ii", 0, 28), A("ii", 56, 84), OP.add)
    ts(A("KF", 0, 28), A("KF", 0, 28), 0.25, OP.mult)
    phys(A("KL", 0, 7), A("ML", 0, 7), A("KF", 0, 7))
    tt(A("DK", 0, 7), A("KF", 0, 7), A("KL", 0, 7), OP.subtract)
    cp(A("PL", 0, 28), A("pi", 0, 28))

    def masks():
        fill(A("MR", 0, 384), 0.0)
        for k in MASKS:
            j, a, b, val = MASKS[k]
            fill(A("MR", 32 * j + a, 32 * j + b), val)
        tr(A("MT", 0, 384), A("MR", 0, 384))

    def more_constants():
        for k in range(4):
            s = 4 * ((16 - 4 * k) % 16)
            for a in range(4):
                act(A("cl", 512 * k + 128 * a, 512 * k + 128 * a + 128, 1, 32 * a, 32 * a + 32), A("cb", s + 128 * a, s + 128 * a + 128, 1, 32 * a, 32 * a + 32))
        fill(A("G", 0, TW), 0.0)
        fill(A("WQ", 0, TW), 0.0)
        quant(A("qcb", 0, 144), A("scb", 0, 144), A("cb", 0, 576))

    def never(name, a, b, val):
        aff(A(name, a, b), A("IOT", 0, b - a), [[0, b - a]], OP.is_equal, val, 1, 0)

    iota(A("IOT", 0, C), [[1, C]], 0, 0)
    never("DR", 0, 320, BIG)
    never("DR", 320, 640, BIG)
    aff(A("gm", 0, 8), A("one", 0, 8), [[-16, 8]], OP.is_ge, 0.0, 0, 1)
    aff(A("gm", 0, 1), A("one", 0, 1), [[0, 1]], OP.is_ge, 0.0, 15, -1)
    aff(A("eb", 0, 516), A("one", 0, 516), [[1, 516]], OP.is_equal, 0.0, -3, -4)
    for c0 in (640, 984, 1328):
        never("DR", c0, min(c0 + 344, 1664), BIG)
    never("CURF", 0, 256, -BIG)
    never("CURF", 256, 512, -BIG)
    for name in ("W1", "W2", "SIG", "OD"):
        n = SCRATCH[name][1][1]
        iota(A(name, 0, n), [[0, n]], 0, 0)
    BLK = [1, 2, 7, 14, 28, 56, 112, 224]

    def resets(late):
        if late:
            fill(A("DR", 640, 1152, 128), -BIG)
            fill(A("DR", 1152, 1664, 256), -BIG)
            return
        for s in (0, 7, 14, 21):
            fill(A("DR", 128 + s, 256, 32), -BIG)
        for s in (0, 14):
            fill(A("DR", 256 + s, 384, 32), -BIG)
        fill(A("DR", 384, 512, 32), -BIG)
        fill(A("DR", 512, 640, 64), -BIG)

    LB, FK = 4, 5

    def counts(bank, ca, cas, cb_, cbs, local, start=True, stop=True):
        for i, k in enumerate((0, 2, 1, 3)):
            s = (16 - 4 * k) % 16
            w, ws = (A("qcl", 128 * k, 128 * k + 128), A("scl", 128 * k, 128 * k + 128)) if local else (A("qcb", s, s + 128), A("scb", s, s + 128))
            c, cs = (ca, cas) if k in (0, 2) else (cb_, cbs)
            o = 2 if k in (2, 3) else 0
            mm(ps(bank, 0, 128), w, ws, A(c, o, o + 128), A(cs, o, o + 128), start and i == 0, stop and i == 3)

    def quant2(tile, ca, cas, cb_, cbs):
        quant(A(ca, 0, 132), A(cas, 0, 132), A(tile, 0, 528))
        quant(A(cb_, 0, 132), A(cbs, 0, 132), A(tile, 4, 532))

    def wrap(dst, row, part=2):
        if part != 1:
            tr(A("TT", 0, C), A(row, 0, C))
            tr(A("TT", C, 2 * C), A(row, 16, 16 + C))
        if part == 0:
            return
        ts(A("CA", 0, 28), A("TT", 0, 896, 32), mask("lo"), OP.mult)
        ts(A("CB", 0, 28), A("TT", 16, 896, 32), mask("hi"), OP.mult)
        tt(A("CD", 0, 28), A("CA", 0, 28), A("CB", 0, 28), OP.add)
        cp(A(dst, 0, 28, 2), A("CD", 0, 14))
        cp(A(dst, 1, 28, 2), A("CD", 14, 28))

    SBANK = [0, 1, 2, 3, 6, 7, 0, 1]
    DBANK = [2, 3, 6, 7]
    PBANK = [0, 1, 4, 2]
    dst = T.cores[(rank + 1) % len(T.cores)]
    rel = _relays(topo, core, dst)
    eng = topo.engines(core, rel[0])
    cut = [eng[:len(eng) // 2], eng[len(eng) // 2:]]
    landed = 2 * sum(len(topo.engines(r, core)) for r in _relays(topo, T.cores[rank - 1], core))

    for t in range(ROUNDS):
        qx, sx, qp, sp = "qx%d" % t, "sx%d" % t, "qp%d" % t, "sp%d" % t
        quant(A(qx, 0, C), A(sx, 0, C), A("xt" if t == 0 else "xn", 0, 1792))
        for i in range(2):
            pick(qp, sp, (HALF * i, HALF * i + HALF), qx, sx, C, A("PL", 14 * i, 14 * i + 14))
        if t == 0:
            quant(A("qu", 0, 128), A("su", 0, 128), A("ut", 0, 512))
        for h in range(2):
            if t == 0:
                repeat_u(h)
            for i, bank in enumerate(((0, 4), (1, 5))[h]):
                o = (HALF * i, HALF * i + HALF)
                mm(ps(bank, 0, HALF), A("qB", 128 * h, 128 * h + 128), A("sB", 128 * h, 128 * h + 128), A(qp, *o), A(sp, *o))
        if t == 0:
            masks()
        for h in range(2):
            for i, bank in enumerate(((0, 4), (1, 5))[h]):
                for a in (2 * i, 2 * i + 1):
                    out, in_ = A("BQ", 112 * h, 112 * h + 112, 1, 32 * a, 32 * a + 32), ps(bank, 112 * (a % 2), 112 * (a % 2) + 112, 1, 32 * a, 32 * a + 32)
                    if i == 0:
                        act(out, in_, only(a))
                    else:
                        ts(out, in_, only(a), OP.mult)

        def scores(h):
            mm(ps(SBANK[h], 0, C), A("qB", 128 * h, 128 * h + 128), A("sB", 128 * h, 128 * h + 128), A(qp, 0, C), A(sp, 0, C))

        def evac(h):
            if h > 5:
                act(A("BF", C * (h - 6), C * (h - 5)), ps(SBANK[h], 0, C))
                return
            for a in range(4):
                act(A("BQ", 112 * h, 112 * h + 112, 1, 32 * a, 32 * a + 32), ps(SBANK[h], 112 * a, 112 * a + 112, 1, 32 * a, 32 * a + 32))

        def unpack(b):
            mm(ps(DBANK[b], 0, C), A("qe", 128 * b, 128 * b + 128), A("se", 128 * b, 128 * b + 128), A(qp, 0, C), A(sp, 0, C))
            act(A("HB", C * b, C * b + C), ps(DBANK[b], 0, C), 0.5)
            if b < 2:
                act(A("FB", C * b, C * b + C), ps(DBANK[b], 0, C))

        if t == 0:
            more_constants()
            repeat_u(2)
        scores(2)
        evac(2)

        def background(lev):
            if t == 0:
                if lev < 6:
                    repeat_u(lev + 2)
                if lev == 1:
                    for b in range(4):
                        quant(A("qe", 128 * b, 128 * b + 128), A("se", 128 * b, 128 * b + 128), A("eb", 3 - b, 515 - b))
                    act(A("COL", 0, C), ind(A("IOT", 0, C), A("PL", 0, 28)))
                if lev == 5:
                    resets(True)
                    ts(A("ii", 0, 8), A("ii", 28, 36), 96, OP.bitwise_and)
                    tt(A("ii", 0, 8), A("ii", 0, 8), A("ii", 84, 92), OP.add)
                    tt(A("ii", 0, 8), A("ii", 0, 8), A("ii", 56, 64), OP.add)
                    cp(A("UL", 64, 72), A("ii", 0, 8))
                    quant(A("qv", 0, 128), A("pv", 0, 128), A("vt", 0, 512))
            scores(lev + 2)
            evac(lev + 2)
            if lev in (4, 5):
                unpack(2 * (lev - 4))
                unpack(2 * (lev - 4) + 1)

        def keep(lev):
            f = ps(FK, 0, 112, 4)
            ts(A("CT", 0, 28), f, A("gm", lev, lev + 1), OP.mult)
            if 0 < lev < 5:
                tt(A("XF", 0, 28), f, A("XF" if lev > 1 else "KF", 0, 28), OP.add)
            tt(A("CK", 0, 28), A("CK" if lev else "KF", 0, 28), A("CT", 0, 28), OP.add)

        def spread(src, lev, c0=0):
            for a in range(4):
                (cp if a < 2 or lev in (0, 5) else act)(A("WQ", 112 * a, 112 * a + 112, 1, 32 * a, 32 * a + 32), A(src, c0, c0 + 112, 1, 32 * a, 32 * a + 32))

        V = lambda n: A("TMP", 56 * n, 56 * n + 56)
        L = lambda n: A("TMP", 56 * n, 56 * n + 56, 2)
        R = lambda n: A("TMP", 56 * n + 1, 56 * n + 56, 2)
        H = lambda n: A("TMP", 28 * n, 28 * n + 28)
        s0, s1 = [[A("BQ", 112 * h + i, 112 * h + 112, 2) for i in range(2)] for h in range(2)]
        tt(V(0), s0[1], s0[0], OP.is_lt)
        tt(V(1), s1[0], s1[1], OP.max)
        ts(V(2), V(0), -2 * BIG, OP.mult, BIG, OP.add)
        ts(V(3), V(0), 2 * BIG, OP.mult, -BIG, OP.add)
        cp(A("G", 256, 368, 2), V(0))
        ts(A("G", 257, 368, 2), V(0), -1.0, OP.mult)
        tt(V(2), s1[0], V(2), OP.min)
        tt(V(3), s1[1], V(3), OP.min)
        if t == 0:
            fill(A("CUR", 0, 128), -BIG)
            fill(A("MC", 0, 128), 0.0)
        tt(V(4), V(2), V(3), OP.max)
        if t == 0:
            resets(False)
        tt(H(10), L(4), R(4), OP.is_gt)
        tt(H(11), L(4), R(1), OP.is_gt)
        tt(H(12), L(1), R(4), OP.is_gt)
        tt(H(13), L(1), R(1), OP.is_gt)
        tt(H(14), H(10), H(11), OP.add)
        tt(H(15), H(12), H(13), OP.add)
        tt(H(16), H(10), H(12), OP.add)
        tt(H(17), H(11), H(13), OP.add)
        tt(H(18), H(15), H(14), OP.subtract)
        tt(H(19), H(17), H(16), OP.subtract)
        tt(H(20), H(14), L(0), OP.add)
        tt(H(21), H(15), L(0), OP.subtract)
        tt(H(22), R(0), H(16), OP.subtract)
        tt(H(23), H(17), R(0), OP.add)
        tt(H(18), H(18), L(0), OP.mult)
        tt(H(19), H(19), R(0), OP.mult)
        tt(A("G", 0, 112, 4), H(20), H(18), OP.add)
        tt(A("G", 1, 112, 4), H(21), H(18), OP.subtract)
        tt(A("G", 2, 112, 4), H(22), H(19), OP.subtract)
        tt(A("G", 3, 112, 4), H(19), H(23), OP.subtract)
        if t == 0:
            for k in range(4):
                quant(A("qcl", 128 * k, 128 * k + 128), A("scl", 128 * k, 128 * k + 128), A("cl", 512 * k, 512 * k + 512))
        quant2("G", "ga", "gas", "gb", "gbs")
        counts(LB, "ga", "gas", "gb", "gbs", True)
        spread("G", 0, 256)
        quant2("WQ", "wa", "was", "wb", "wbs")
        counts(FK, "wa", "was", "wb", "wbs", False)
        spread("G", 0)
        tt(A("XL", 0, 7), ps(LB, 0, 28, 4), A("KL", 0, 7), OP.add)
        ts(A("LL", 0, 7), A("XL", 0, 7), 4.0, OP.mult)
        background(1)

        for lev in range(2, 6):
            scatter(A("CUR", 0, 128), A("LL", 0, 7), A("BQ", 112 * lev, 112 * lev + 112))
            if lev == 2:
                keep(0)
                quant2("WQ", "wa", "was", "wb", "wbs")
                counts(FK, "wa", "was", "wb", "wbs", False)
            scan(A("KEY", 0, 128), A("DR", 128 * (lev - 1), 128 * lev), A("CUR", 0, 128))
            tr(A("TQ", 0, 128), A("KEY", 0, 128))
            one = lambda b: A("TQ", 32 * b, 32 * b + 1)
            if lev in (2, 3):
                w = BLK[lev]
                for b in range(4):
                    for j in range(28 // w):
                        a = 32 * b + w * j
                        ts(A("MC", a, a + w), A("KEY", a, a + w), one(b), OP.is_lt if j % 2 else OP.is_gt, mask(("b%d" if lev == 2 else "c%d") % j), OP.mult)
            elif lev == 4:
                for b in range(4):
                    a = 32 * b
                    ts(A("MC", a, a + 32), A("KEY", a, a + 32), one(b ^ 1), OP.is_lt if b % 2 else OP.is_gt, mask("n" if b % 2 else "p"), OP.mult)
            else:
                for i, m in enumerate(("MC", "MC2")):
                    ts(A(m, 0, 64), A("KEY", 0, 64), one(2 + i), OP.is_gt, mask("p"), OP.mult)
                    ts(A(m, 64, 128), A("KEY", 64, 128), one(i), OP.is_lt, mask("n"), OP.mult)
                tt(A("MC", 0, 128), A("MC", 0, 128), A("MC2", 0, 128), OP.add)
            cp(A("G", 0, 112), ind(A("MC", 0, 128), A("LL", 0, 7)))
            if lev < 5:
                quant2("G", "ga", "gas", "gb", "gbs")
                counts(LB, "ga", "gas", "gb", "gbs", True)
            spread("G", lev)
            keep(lev - 1)
            if lev == 4:
                tt(A("XK", 0, 7), A("XL", 0, 7), A("DK", 0, 7), OP.add)
            quant2("WQ", "wa", "was", "wb", "wbs")
            counts(FK, "wa", "was", "wb", "wbs", False)
            if lev < 5:
                loc = ps(LB, 0, 28, 4)
                if lev < 4:
                    tt(A("XL", 0, 7), loc, A("XL", 0, 7), OP.add)
                    ts(A("LL", 0, 7), A("XL", 0, 7), 4.0, OP.mult)
                else:
                    tt(A("XL", 0, 7), loc, A("XK", 0, 7), OP.add)
                    phys(A("YL", 0, 7), A("ML", 0, 7), A("XL", 0, 7))
                    ts(A("LL", 0, 7), A("YL", 0, 7), 4.0, OP.mult)
            background(lev)

        if t == ROUNDS - 1:
            scatter(A("OD", 0, 480), A("R2", 0, 28), A("COL", C * t - C, C * t))
        for lev in (6, 7):
            tt(A("XF", 0, 28), ps(FK, 0, 112, 4), A("XF", 0, 28), OP.add)
            phys(A("YF", 0, 28), A("MF", 0, 28), A("XF", 0, 28))
            ts(A("LF", 0, 28), A("YF", 0, 28), 4.0, OP.mult)
            scatter(A("CURF", 0, 512), A("LF", 0, 28), A("BF", C * (lev - 6), C * (lev - 5)))
            scan(A("KEYF", 0, 512), A("DR", 640 + 512 * (lev - 6), 1152 + 512 * (lev - 6)), A("CURF", 0, 512))
            cp(A("TMP", 0, 128), ind(A("KEYF", 0, 512), A("UL", 64, 72)))
            tr(A("TF", 0, 128), A("TMP", 0, 128))
            one = lambda s: A("TF", 32 * s, 32 * s + 1)
            if lev == 6:
                for s in range(4):
                    ts(A("MCF", 128 * s, 128 * s + 128), A("KEYF", 128 * s, 128 * s + 128), one(s ^ 1), OP.is_lt if s % 2 else OP.is_gt, mask("n" if s % 2 else "p"), OP.mult)
            else:
                for i, m in ((1, "MCG"), (0, "MCF")):
                    ts(A(m, 0, 256), A("KEYF", 0, 256), one(2 + i), OP.is_gt, mask("p"), OP.mult)
                    ts(A(m, 256, 512), A("KEYF", 256, 512), one(i), OP.is_lt, mask("n"), OP.mult)
                    if i:
                        act(A("W2", 0, C), ind(A(m, 0, 512), A("LF", 0, 28)))
            cp(A("W1", 0, C), ind(A("MCF", 0, 512), A("LF", 0, 28)))
            keep(lev - 1)
            quant2("W1", "wa", "was", "wb", "wbs")
            counts(FK, "wa", "was", "wb", "wbs", False, True, lev == 6)
            if lev == 7:
                quant2("W2", "ga", "gas", "gb", "gbs")
                counts(FK, "ga", "gas", "gb", "gbs", False, False, True)
            if t == ROUNDS - 1:
                wrap("CW", "OD", lev - 6)
        keep(7)
        ts(A("RL", 0, 28), A("CK", 0, 28), 4.0, OP.mult, mask("h16"), OP.add)
        scatter(A("SIG", 0, 480), A("RL", 0, 28), A("IOT", 0, C))
        wrap("ZL", "SIG")

        for b in range(4):
            (act if b else cp)(A("GZ", HALF * b, HALF * b + HALF), ind(A("HB", C * b, C * b + C), A("ZL", 0, 14)))
        for b in range(4):
            tt(A("ZT", b, 896, 4), ind(A("HB", C * b, C * b + C), A("ZL", 14, 28)), A("GZ", HALF * b, HALF * b + HALF), OP.add)
        zc, zs = "zc%d" % t, "zs%d" % t
        quant(A(zc, 0, HALF), A(zs, 0, HALF), A("ZT", 0, 896))

        hazards("g", [(zc, 0, 128, 0, HALF, 1), (zs, 0, 128, 0, HALF, 1)], [])
        for nm, hn, sn in ((zc, "hc%d" % t, "rc%d" % t), (zs, "hs%d" % t, "rs%d" % t)):
            tf = []
            for i in range(2):
                rid, pid = topo.addr(rel[i], core)
                s_, d_ = T[nm][:, i * HALF // 2:(i + 1) * HALF // 2], T[hn][:, :]
                if nm == zc:
                    s_, d_ = s_.bitcast(dt.uint8), d_.bitcast(dt.uint8)
                tf.append(RemoteDMATransfer(dst_ids=[DstId(rid=rid, pnc=pid)], dma_engine_mask=_bits(cut[i]), remote_sem=T.sem[sn], src=s_, dst=d_))
            g.remote_dma_fused(tf, local_sem=T.sem.snd)

        ts(A("CT", 0, 28), A("CK", 0, 28), 56.0, OP.is_ge, -56.0, OP.mult)
        tt(A("CA", 0, 28), A("CK", 0, 28), A("CT", 0, 28), OP.add)
        ts(A("RM", 0, 28), A("CA", 0, 28), 4.0, OP.mult)
        now = A("COL", C * t, C * t + C)
        if t < ROUNDS - 1:
            tt(A("KT", 0, 28), ps(FK, 0, 112, 4), A("XF", 0, 28), OP.add)
            ts(A("R2", 0, 28), A("KT", 0, 28), 4.0, OP.mult, mask("h16"), OP.add)
            scatter(A("SIG", 0, 480), A("R2", 0, 28), A("IOT", 0, C))
            wrap("PL", "SIG")
        else:
            ts(A("R2", 0, 28), A("CW", 0, 28), mask("h16"), OP.add)
            scatter(A("SIG", 0, 480), A("R2", 0, 28), A("IOT", 0, C))
            wrap("IC", "SIG")

        lc, ls = "lc%d" % t, "ls%d" % t
        wait("t", "lz%d" % t, landed)
        for b in (2, 0, 3, 1):
            mm(ps(PBANK[b], 0, HALF), A("wq", 128 * b, 128 * b + 128), A("wp", 128 * b, 128 * b + 128), A(lc, 0, HALF), A(ls, 0, HALF))
            act(A("PB", HALF * b, HALF * b + HALF), ps(PBANK[b], 0, HALF), 0.03125)
        for b in (2, 3):
            act(A("RG", C * (b - 2), C * (b - 1)), ind(A("PB", HALF * b, HALF * b + HALF), A("RM", 0, 28)))
        if t < ROUNDS - 1:
            act(A("COL", C * t + C, C * t + 2 * C), ind(now, A("PL", 0, 28)))
        for b in (0, 1):
            tt(A("xn", b, 1792, 4), ind(A("PB", HALF * b, HALF * b + HALF), A("RM", 0, 28)), A("FB", C * b, C * b + C), OP.add)
        for b in (2, 3):
            tt(A("xn", b, 1792, 4), A("RG", C * (b - 2), C * (b - 1)), ps(DBANK[b], 0, C), OP.add)

    quant(A("qx3", 0, C), A("sx3", 0, C), A("xn", 0, 1792))
    pick("qp3", "sp3", (0, C), "qx3", "sx3", C, A("IC", 0, 28))
    mm(ps(0, 0, C), A("qv", 0, 128), A("pv", 0, 128), A("qp3", 0, C), A("sp3", 0, C))
    dmas("y", [(ext(T.oc[:, :]), bc(A("qp3", 0, C)))], "dc")
    dmas("s", [(ext(T.osc[4 * k:4 * k + 4, :]), A("sp3", 0, C, 1, 32 * k, 32 * k + 4)) for k in range(4)], "dq")
    cp(A("yb", 0, C), ps(0, 0, C))
    dmas("y", [(ext(T.y[:, :]), A("yb", 0, C))], "dy")
    scatter(A("OD", 0, 480), A("RL", 0, 28), A("COL", C * t, C * t + C))
    dmas("s", [(ext(T.od[h:h + 1, :]), A("OD", 16 * (h % 2), 16 * (h % 2) + C, 1, 16 * h, 16 * h + 1)) for h in range(8)], "dd")
    for sem in count:
        wait("g", sem, count[sem])
    wait("g", "snd", 2 * len(eng) * ROUNDS)
